import numpy as np
import ml_dtypes


def mxq(x, axis, fmt="e4m3"):
    dtype, down = {"e4m3": (ml_dtypes.float8_e4m3fn, 7), "e5m2": (ml_dtypes.float8_e5m2, 14)}[fmt]
    v = np.moveaxis(np.asarray(x, np.float32).astype(ml_dtypes.bfloat16).astype(np.float64), axis, -1)
    blocks = v.reshape(v.shape[:-1] + (-1, 32))
    amax = np.abs(blocks).max(-1, keepdims=True)
    byte = np.maximum(np.where(amax > 0, np.frexp(amax)[1] - 1 + 127, 0) - down, 1)
    scale = np.exp2(byte - 127.0)
    codes = (blocks / scale).astype(np.float32).astype(dtype).astype(np.float64)
    return np.moveaxis((codes * scale).reshape(v.shape), -1, axis)


WIDE = False


def mx_kscale(k):
    if not WIDE:
        return np.ones(k)
    levels = np.array([10, -10, 5, -5, 0])
    if k % 512:
        return np.exp2(np.random.permutation(np.resize(levels, k // 32))).repeat(32)
    a = np.empty((k // 512, 16))
    for p in range(k // 512):
        a[p, :8] = np.random.permutation(np.resize(levels, 8))
        for g in range(8):
            far = levels[np.abs(levels - a[p, g]) >= 10]
            a[p, g + 8] = far[np.random.randint(len(far))]
    return np.exp2(a.ravel()).repeat(32)


def f64(x):
    return np.asarray(x).astype(np.float64)


def striped(idx):
    return np.tile(np.asarray(idx).reshape(-1, 16).T, (8, 1)).astype(np.uint16)


def unstriped(offs):
    return offs[:16].T.reshape(-1).astype(np.int64)


E2M1 = np.array([0.0, 0.5, 1.0, 1.5, 2.0, 3.0, 4.0, 6.0, -0.0, -0.5, -1.0, -1.5, -2.0, -3.0, -4.0, -6.0])


def pack_weight(w, fmt):
    k, n = w.shape
    w = f64(np.asarray(w, np.float32).astype(ml_dtypes.bfloat16)).reshape(k // 32, 32, n)
    amax = np.abs(w).max(1)
    if fmt == "e4m3":
        byte = np.frexp(amax)[1] - 1 + 127 - 7
    else:
        mant, ex = np.frexp(amax / 6.0)
        byte = np.where(mant > 0.5, ex, ex - 1) + 127
    byte = np.clip(np.where(amax > 0, byte, 1), 1, 254)
    scaled = (w * np.exp2(127.0 - byte)[:, None, :]).reshape(k, n).astype(np.float32)
    by_word = np.ascontiguousarray(scaled.reshape(k // 512, 128, 4, n).transpose(0, 1, 3, 2))
    if fmt == "e4m3":
        words = by_word.astype(ml_dtypes.float8_e4m3fn).view(np.uint8)
    else:
        c = by_word.astype(ml_dtypes.float4_e2m1fn).view(np.uint8) & 0xF
        words = (c[..., 0::2] | (c[..., 1::2] << 4)).reshape(k // 512, 128, 2 * n)
    return np.ascontiguousarray(words), np.ascontiguousarray(byte.astype(np.uint8).reshape(k // 512, 16, n))


def unpack_weight(words, scales, fmt):
    g, _, n = scales.shape
    words = np.ascontiguousarray(words).reshape(g, 128, n, -1)
    if fmt == "e4m3":
        vals = words.view(ml_dtypes.float8_e4m3fn).astype(np.float64)
    else:
        nib = np.empty((g, 128, n, 4), np.uint8)
        nib[..., 0::2] = words & 0xF
        nib[..., 1::2] = words >> 4
        vals = E2M1[nib]
    vals = vals * np.repeat(np.exp2(scales.astype(np.float64) - 127.0), 8, axis=1)[..., None]
    return vals.transpose(0, 1, 3, 2).reshape(g * 512, n)


B, N, T, D, NQ = 1, 512, 2048, 512, 256


def setup_inputs():
    n = np.random.standard_normal
    idx = np.random.permutation(T)[:B * N]
    s = mx_kscale(D)[:, None]
    kp = pack_weight(n((D, T)) / s, "e4m3")
    return {
        "qT": (n((B, D, NQ)) * s * (1.00 / np.sqrt(D))).astype(np.float32),
        "k_words": kp[0],
        "k_scales": kp[1],
        "kn": np.tile(np.random.uniform(1.0, 4.0, 2048), (128, 1)).astype(np.float32),
        "qn": (np.random.uniform(1.0, 4.0, (B, NQ, 1))).astype(np.float32),
        "offs": striped(idx),
    }


def reference(qT, k_words, k_scales, kn, qn, offs):
    idx = unstriped(offs)
    pick = lambda x, which: x[:, which].reshape(x.shape[0], B, -1).transpose(1, 0, 2)
    k = unpack_weight(k_words, k_scales, "e4m3")
    kg = pick(k, idx)
    qq = mxq(f64(qT), 1, "e4m3")
    a = qq.transpose(0, 2, 1) @ kg
    y = np.maximum(f64(qn) + pick(f64(kn), idx)[:, :1, :] - 2.0 * a, 0.0)
    return y

@@ -1,0 +1,121 @@
+from contextlib import ExitStack
+
+import concourse.mybir as mybir
+from concourse.masks import make_identity
+
+N, T, D, NQ = 512, 2048, 512, 256
+FLOPS = 2 * NQ * N * D
+BYTES = 4 * D * NQ + D * T + 16 * T + 4 * T + 4 * NQ + 2 * 128 * (N // 16) + 4 * NQ * N
+
+F32 = mybir.dt.float32
+BF16 = mybir.dt.bfloat16
+I32 = mybir.dt.int32
+U32 = mybir.dt.uint32
+U16 = mybir.dt.uint16
+U8 = mybir.dt.uint8
+FP8X4 = mybir.dt.float8_e4m3fn_x4
+ALU = mybir.AluOpType
+ACT = mybir.ActivationFunctionType
+
+P = 128
+PACK = 4
+HALF = N // 2
+KN_ROW = P - 1
+SPLIT = 1280
+
+
+def tile_attend_infodist_topk_kernel(tc, qT, k_words, k_scales, kn, qn, offs, out):
+    nc = tc.nc
+    with ExitStack() as ctx:
+        sb = ctx.enter_context(tc.tile_pool(name="sb", bufs=1))
+        ps = ctx.enter_context(tc.psum_pool(name="ps", bufs=1))
+
+        offsets = sb.tile([P, N // 16], U16, name="offsets")
+        scale_pool = sb.tile([P, T], U8, name="scale_pool", align_bytes=64)
+        kn_pool = sb.tile([P, T], F32, name="kn_pool", align_bytes=64)
+        word_pool = sb.tile([P, T], U32, name="word_pool", align_bytes=64)
+        q_raw = [
+            sb.tile([P, PACK, P], F32, name="q_raw%d" % h, tag="q_raw%d" % h, align_bytes=64)
+            for h in range(2)
+        ]
+        qn_cols = sb.tile([P, 2], F32, name="qn_cols")
+        ident = sb.tile([P, P], F32, name="ident", align_bytes=64)
+
+        nc.vector.memset(scale_pool[:].bitcast(I32), 0)
+        nc.gpsimd.memset(kn_pool[0:KN_ROW, 0:SPLIT], 0.0)
+        nc.vector.memset(kn_pool[0:KN_ROW, SPLIT:T], 0.0)
+        make_identity(nc, ident[:])
+
+        nc.sync.dma_start(offsets[:], offs)
+        nc.sync.dma_start(kn_pool[KN_ROW:P, :], kn[0:1, :])
+        for quad in range(4):
+            nc.sync.dma_start(
+                scale_pool[32 * quad : 32 * quad + 4, :].bitcast(I32),
+                k_scales[0, 4 * quad : 4 * quad + 4, :].bitcast(I32),
+            )
+        nc.sync.dma_start(
+            word_pool[:].bitcast(I32),
+            k_words[0].rearrange("p n t -> p (n t)").bitcast(I32),
+        )
+        q_rows = qT[0].rearrange("(p j) q -> p j q", j=PACK)
+        for h in range(2):
+            nc.sync.dma_start(q_raw[h][:], q_rows[:, :, P * h : P * (h + 1)])
+        with nc.allow_non_contiguous_dma(reason="one number a query row"):
+            nc.sync.dma_start(qn_cols[:], qn[0].rearrange("(h m) o -> m (h o)", h=2))
+
+        kn_listed = sb.tile([P, N], F32, name="kn_listed", tag="grouped0", align_bytes=64)
+        nc.vector.tensor_copy(kn_listed[:], kn_pool[:].indirect(offsets[:]))
+        k_planes = sb.tile([P, N], U8, name="k_planes", align_bytes=64)
+        nc.vector.tensor_copy(k_planes[:], scale_pool[:].indirect(offsets[:]))
+
+        turned = ps.tile([P, 4, P], F32, name="turned")
+        for j in range(4):
+            nc.tensor.transpose(turned[:, j, :], kn_listed[:, P * j : P * (j + 1)], ident[:])
+        kn_cols = sb.tile([P, 4], F32, name="kn_cols")
+        nc.scalar.copy(kn_cols[:], turned[:, :, KN_ROW])
+        spread = ps.tile([P, N], F32, name="spread")
+        for j in range(4):
+            nc.tensor.transpose(
+                spread[:, P * j : P * (j + 1)], kn_cols[:, j : j + 1].to_broadcast([P, P]), ident[:]
+            )
+
+        k_codes = sb.tile([P, N], U32, name="k_codes", align_bytes=64)
+        nc.vector.tensor_copy(k_codes[:], word_pool[:].indirect(offsets[:]))
+
+        accs = []
+        for h in range(2):
+            grouped = sb.tile([P, P, PACK], BF16, name="grouped%d" % h, tag="grouped%d" % h, align_bytes=64)
+            woven = q_raw[h][:].rearrange("p j m -> p m j")
+            nc.scalar.activation(grouped[:], woven, ACT.Copy)
+            codes = sb.tile([P, P], U32, name="q_codes%d" % h, align_bytes=64)
+            plane = sb.tile([P, P], U8, name="q_plane%d" % h, align_bytes=64)
+            nc.vector.quantize_mx(
+                out=codes[:].bitcast(FP8X4),
+                scales=plane[:],
+                in_=grouped[:].rearrange("p m j -> p (m j)"),
+            )
+            acc = ps.tile([P, N], F32, name="acc%d" % h)
+            nc.tensor.matmul_mx(
+                out=acc[:],
+                lhsT=codes[:].bitcast(FP8X4),
+                lhsT_scale=plane[:],
+                rhs=k_codes[:].bitcast(FP8X4),
+                rhs_scale=k_planes[:],
+                start=True,
+                stop=True,
+            )
+            accs.append(acc)
+
+        kn_rows = sb.tile([P, N], F32, name="kn_rows", tag="q_raw0", align_bytes=64)
+        nc.vector.tensor_copy(kn_rows[:], spread[:])
+
+        for h in range(2):
+            for c in range(2):
+                slots = slice(c * HALF, (c + 1) * HALF)
+                part = sb.tile([P, HALF], F32, name="part%d%d" % (c, h), align_bytes=64)
+                nc.vector.scalar_tensor_tensor(
+                    part[:], accs[h][:, slots], -2.0, kn_rows[:, slots], ALU.mult, ALU.add
+                )
+                res = sb.tile([P, HALF], F32, name="res%d%d" % (c, h), align_bytes=64)
+                nc.scalar.activation(res[:], part[:], ACT.Relu, bias=qn_cols[:, h : h + 1])
+                nc.sync.dma_start(out[0, P * h : P * (h + 1), slots], res[:])

@@ -21,7 +21,6 @@ P = 128
 PACK = 4
 HALF = N // 2
 KN_ROW = P - 1
-SPLIT = 1280
 
 
 def tile_attend_infodist_topk_kernel(tc, qT, k_words, k_scales, kn, qn, offs, out):
@@ -34,20 +33,17 @@ def tile_attend_infodist_topk_kernel(tc, qT, k_words, k_scales, kn, qn, offs, ou
         scale_pool = sb.tile([P, T], U8, name="scale_pool", align_bytes=64)
         kn_pool = sb.tile([P, T], F32, name="kn_pool", align_bytes=64)
         word_pool = sb.tile([P, T], U32, name="word_pool", align_bytes=64)
-        q_raw = [
-            sb.tile([P, PACK, P], F32, name="q_raw%d" % h, tag="q_raw%d" % h, align_bytes=64)
-            for h in range(2)
-        ]
+        q_raw = sb.tile([P, PACK, NQ], F32, name="q_raw", tag="q_raw", align_bytes=64)
         qn_cols = sb.tile([P, 2], F32, name="qn_cols")
         ident = sb.tile([P, P], F32, name="ident", align_bytes=64)
 
         nc.vector.memset(scale_pool[:].bitcast(I32), 0)
-        nc.gpsimd.memset(kn_pool[0:KN_ROW, 0:SPLIT], 0.0)
-        nc.vector.memset(kn_pool[0:KN_ROW, SPLIT:T], 0.0)
+        nc.vector.memset(kn_pool[0:KN_ROW, :], 0.0)
         make_identity(nc, ident[:])
 
         nc.sync.dma_start(offsets[:], offs)
         nc.sync.dma_start(kn_pool[KN_ROW:P, :], kn[0:1, :])
+        nc.sync.dma_start(q_raw[:], qT[0].rearrange("(p j) q -> p j q", j=PACK))
         for quad in range(4):
             nc.sync.dma_start(
                 scale_pool[32 * quad : 32 * quad + 4, :].bitcast(I32),
@@ -57,36 +53,20 @@ def tile_attend_infodist_topk_kernel(tc, qT, k_words, k_scales, kn, qn, offs, ou
             word_pool[:].bitcast(I32),
             k_words[0].rearrange("p n t -> p (n t)").bitcast(I32),
         )
-        q_rows = qT[0].rearrange("(p j) q -> p j q", j=PACK)
-        for h in range(2):
-            nc.sync.dma_start(q_raw[h][:], q_rows[:, :, P * h : P * (h + 1)])
         with nc.allow_non_contiguous_dma(reason="one number a query row"):
             nc.sync.dma_start(qn_cols[:], qn[0].rearrange("(h m) o -> m (h o)", h=2))
 
-        kn_listed = sb.tile([P, N], F32, name="kn_listed", tag="grouped0", align_bytes=64)
+        kn_listed = sb.tile([P, N], F32, name="kn_listed", align_bytes=64)
         nc.vector.tensor_copy(kn_listed[:], kn_pool[:].indirect(offsets[:]))
         k_planes = sb.tile([P, N], U8, name="k_planes", align_bytes=64)
         nc.vector.tensor_copy(k_planes[:], scale_pool[:].indirect(offsets[:]))
 
-        turned = ps.tile([P, 4, P], F32, name="turned")
-        for j in range(4):
-            nc.tensor.transpose(turned[:, j, :], kn_listed[:, P * j : P * (j + 1)], ident[:])
-        kn_cols = sb.tile([P, 4], F32, name="kn_cols")
-        nc.scalar.copy(kn_cols[:], turned[:, :, KN_ROW])
-        spread = ps.tile([P, N], F32, name="spread")
-        for j in range(4):
-            nc.tensor.transpose(
-                spread[:, P * j : P * (j + 1)], kn_cols[:, j : j + 1].to_broadcast([P, P]), ident[:]
-            )
-
-        k_codes = sb.tile([P, N], U32, name="k_codes", align_bytes=64)
-        nc.vector.tensor_copy(k_codes[:], word_pool[:].indirect(offsets[:]))
-
-        accs = []
+        q_codes, q_planes = [], []
         for h in range(2):
-            grouped = sb.tile([P, P, PACK], BF16, name="grouped%d" % h, tag="grouped%d" % h, align_bytes=64)
-            woven = q_raw[h][:].rearrange("p j m -> p m j")
-            nc.scalar.activation(grouped[:], woven, ACT.Copy)
+            grouped = sb.tile([P, P, PACK], BF16, name="grouped%d" % h, align_bytes=64)
+            nc.scalar.activation(
+                grouped[:], q_raw[:, :, P * h : P * (h + 1)].rearrange("p j m -> p m j"), ACT.Copy
+            )
             codes = sb.tile([P, P], U32, name="q_codes%d" % h, align_bytes=64)
             plane = sb.tile([P, P], U8, name="q_plane%d" % h, align_bytes=64)
             nc.vector.quantize_mx(
@@ -94,27 +74,45 @@ def tile_attend_infodist_topk_kernel(tc, qT, k_words, k_scales, kn, qn, offs, ou
                 scales=plane[:],
                 in_=grouped[:].rearrange("p m j -> p (m j)"),
             )
-            acc = ps.tile([P, N], F32, name="acc%d" % h)
-            nc.tensor.matmul_mx(
-                out=acc[:],
-                lhsT=codes[:].bitcast(FP8X4),
-                lhsT_scale=plane[:],
-                rhs=k_codes[:].bitcast(FP8X4),
-                rhs_scale=k_planes[:],
-                start=True,
-                stop=True,
+            q_codes.append(codes)
+            q_planes.append(plane)
+
+        turned = ps.tile([P, 4, P], F32, name="turned")
+        for j in range(4):
+            nc.tensor.transpose(turned[:, j, :], kn_listed[:, P * j : P * (j + 1)], ident[:])
+        kn_cols = sb.tile([P, 4], F32, name="kn_cols", tag="q_raw", align_bytes=64)
+        nc.scalar.copy(kn_cols[:], turned[:, :, KN_ROW])
+        spread = ps.tile([P, N], F32, name="spread")
+        for j in range(4):
+            nc.tensor.transpose(
+                spread[:, P * j : P * (j + 1)], kn_cols[:, j : j + 1].to_broadcast([P, P]), ident[:]
             )
-            accs.append(acc)
+        kn_rows = sb.tile([P, N], F32, name="kn_rows", align_bytes=64)
+        nc.scalar.copy(kn_rows[:], spread[:])
 
-        kn_rows = sb.tile([P, N], F32, name="kn_rows", tag="q_raw0", align_bytes=64)
-        nc.vector.tensor_copy(kn_rows[:], spread[:])
+        k_codes = []
+        for c in range(2):
+            listed = sb.tile([P, HALF], U32, name="k_codes%d" % c, align_bytes=64)
+            cols = slice(c * (HALF // 16), (c + 1) * (HALF // 16))
+            nc.vector.tensor_copy(listed[:], word_pool[:].indirect(offsets[:, cols]))
+            k_codes.append(listed)
 
-        for h in range(2):
-            for c in range(2):
-                slots = slice(c * HALF, (c + 1) * HALF)
+        for c in range(2):
+            slots = slice(c * HALF, (c + 1) * HALF)
+            for h in range(2):
+                acc = ps.tile([P, HALF], F32, name="acc%d%d" % (c, h))
+                nc.tensor.matmul_mx(
+                    out=acc[:],
+                    lhsT=q_codes[h][:].bitcast(FP8X4),
+                    lhsT_scale=q_planes[h][:],
+                    rhs=k_codes[c][:].bitcast(FP8X4),
+                    rhs_scale=k_planes[:, slots],
+                    start=True,
+                    stop=True,
+                )
                 part = sb.tile([P, HALF], F32, name="part%d%d" % (c, h), align_bytes=64)
                 nc.vector.scalar_tensor_tensor(
-                    part[:], accs[h][:, slots], -2.0, kn_rows[:, slots], ALU.mult, ALU.add
+                    part[:], acc[:], -2.0, kn_rows[:, slots], ALU.mult, ALU.add
                 )
                 res = sb.tile([P, HALF], F32, name="res%d%d" % (c, h), align_bytes=64)
                 nc.scalar.activation(res[:], part[:], ACT.Relu, bias=qn_cols[:, h : h + 1])

@@ -38,8 +38,9 @@ def tile_attend_infodist_topk_kernel(tc, qT, k_words, k_scales, kn, qn, offs, ou
         ident = sb.tile([P, P], F32, name="ident", align_bytes=64)
 
         nc.vector.memset(scale_pool[:].bitcast(I32), 0)
-        nc.vector.memset(kn_pool[0:KN_ROW, :], 0.0)
-        make_identity(nc, ident[:])
+        nc.vector.memset(kn_pool[0:KN_ROW, :].bitcast(I32), 0)
+        nc.vector.memset(ident[:], 0.0)
+        make_identity(nc, ident[:], nomemset=True)
 
         nc.sync.dma_start(offsets[:], offs)
         nc.sync.dma_start(kn_pool[KN_ROW:P, :], kn[0:1, :])
@@ -61,21 +62,19 @@ def tile_attend_infodist_topk_kernel(tc, qT, k_words, k_scales, kn, qn, offs, ou
         k_planes = sb.tile([P, N], U8, name="k_planes", align_bytes=64)
         nc.vector.tensor_copy(k_planes[:], scale_pool[:].indirect(offsets[:]))
 
-        q_codes, q_planes = [], []
+        grouped = sb.tile([P, NQ, PACK], BF16, name="grouped", align_bytes=64)
         for h in range(2):
-            grouped = sb.tile([P, P, PACK], BF16, name="grouped%d" % h, align_bytes=64)
+            rows = slice(P * h, P * (h + 1))
             nc.scalar.activation(
-                grouped[:], q_raw[:, :, P * h : P * (h + 1)].rearrange("p j m -> p m j"), ACT.Copy
+                grouped[:, rows, :], q_raw[:, :, rows].rearrange("p j m -> p m j"), ACT.Copy
             )
-            codes = sb.tile([P, P], U32, name="q_codes%d" % h, align_bytes=64)
-            plane = sb.tile([P, P], U8, name="q_plane%d" % h, align_bytes=64)
-            nc.vector.quantize_mx(
-                out=codes[:].bitcast(FP8X4),
-                scales=plane[:],
-                in_=grouped[:].rearrange("p m j -> p (m j)"),
-            )
-            q_codes.append(codes)
-            q_planes.append(plane)
+        q_codes = sb.tile([P, NQ], U32, name="q_codes", align_bytes=64)
+        q_plane = sb.tile([P, NQ], U8, name="q_plane", align_bytes=64)
+        nc.vector.quantize_mx(
+            out=q_codes[:].bitcast(FP8X4),
+            scales=q_plane[:],
+            in_=grouped[:].rearrange("p m j -> p (m j)"),
+        )
 
         turned = ps.tile([P, 4, P], F32, name="turned")
         for j in range(4):
@@ -103,8 +102,8 @@ def tile_attend_infodist_topk_kernel(tc, qT, k_words, k_scales, kn, qn, offs, ou
                 acc = ps.tile([P, HALF], F32, name="acc%d%d" % (c, h))
                 nc.tensor.matmul_mx(
                     out=acc[:],
-                    lhsT=q_codes[h][:].bitcast(FP8X4),
-                    lhsT_scale=q_planes[h][:],
+                    lhsT=q_codes[:, P * h : P * (h + 1)].bitcast(FP8X4),
+                    lhsT_scale=q_plane[:, P * h : P * (h + 1)],
                     rhs=k_codes[c][:].bitcast(FP8X4),
                     rhs_scale=k_planes[:, slots],
                     start=True,

@@ -42,8 +42,8 @@ def tile_attend_infodist_topk_kernel(tc, qT, k_words, k_scales, kn, qn, offs, ou
         nc.vector.memset(ident[:], 0.0)
         make_identity(nc, ident[:], nomemset=True)
 
-        nc.sync.dma_start(offsets[:], offs)
         nc.sync.dma_start(kn_pool[KN_ROW:P, :], kn[0:1, :])
+        nc.sync.dma_start(offsets[:], offs)
         nc.sync.dma_start(q_raw[:], qT[0].rearrange("(p j) q -> p j q", j=PACK))
         for quad in range(4):
             nc.sync.dma_start(
@@ -66,7 +66,9 @@ def tile_attend_infodist_topk_kernel(tc, qT, k_words, k_scales, kn, qn, offs, ou
         for h in range(2):
             rows = slice(P * h, P * (h + 1))
             nc.scalar.activation(
-                grouped[:, rows, :], q_raw[:, :, rows].rearrange("p j m -> p m j"), ACT.Copy
+                grouped[:, rows, :].rearrange("p (c i) j -> p c j i", i=4),
+                q_raw[:, :, rows].rearrange("p j (c i) -> p c j i", i=4),
+                ACT.Copy,
             )
         q_codes = sb.tile([P, NQ], U32, name="q_codes", align_bytes=64)
         q_plane = sb.tile([P, NQ], U8, name="q_plane", align_bytes=64)
@@ -81,13 +83,18 @@ def tile_attend_infodist_topk_kernel(tc, qT, k_words, k_scales, kn, qn, offs, ou
             nc.tensor.transpose(turned[:, j, :], kn_listed[:, P * j : P * (j + 1)], ident[:])
         kn_cols = sb.tile([P, 4], F32, name="kn_cols", tag="q_raw", align_bytes=64)
         nc.scalar.copy(kn_cols[:], turned[:, :, KN_ROW])
-        spread = ps.tile([P, N], F32, name="spread")
-        for j in range(4):
-            nc.tensor.transpose(
-                spread[:, P * j : P * (j + 1)], kn_cols[:, j : j + 1].to_broadcast([P, P]), ident[:]
-            )
-        kn_rows = sb.tile([P, N], F32, name="kn_rows", align_bytes=64)
-        nc.scalar.copy(kn_rows[:], spread[:])
+        kn_rows = []
+        for c in range(2):
+            spread = ps.tile([P, HALF], F32, name="spread%d" % c)
+            for j in range(2):
+                nc.tensor.transpose(
+                    spread[:, P * j : P * (j + 1)],
+                    kn_cols[:, 2 * c + j : 2 * c + j + 1].to_broadcast([P, P]),
+                    ident[:],
+                )
+            rows = sb.tile([P, HALF], F32, name="kn_rows%d" % c, align_bytes=64)
+            nc.scalar.copy(rows[:], spread[:])
+            kn_rows.append(rows)
 
         k_codes = []
         for c in range(2):
@@ -111,7 +118,7 @@ def tile_attend_infodist_topk_kernel(tc, qT, k_words, k_scales, kn, qn, offs, ou
                 )
                 part = sb.tile([P, HALF], F32, name="part%d%d" % (c, h), align_bytes=64)
                 nc.vector.scalar_tensor_tensor(
-                    part[:], acc[:], -2.0, kn_rows[:, slots], ALU.mult, ALU.add
+                    part[:], acc[:], -2.0, kn_rows[c][:], ALU.mult, ALU.add
                 )
                 res = sb.tile([P, HALF], F32, name="res%d%d" % (c, h), align_bytes=64)
                 nc.scalar.activation(res[:], part[:], ACT.Relu, bias=qn_cols[:, h : h + 1])

@@ -116,10 +116,25 @@ def tile_attend_infodist_topk_kernel(tc, qT, k_words, k_scales, kn, qn, offs, ou
                     start=True,
                     stop=True,
                 )
-                part = sb.tile([P, HALF], F32, name="part%d%d" % (c, h), align_bytes=64)
-                nc.vector.scalar_tensor_tensor(
-                    part[:], acc[:], -2.0, kn_rows[c][:], ALU.mult, ALU.add
-                )
                 res = sb.tile([P, HALF], F32, name="res%d%d" % (c, h), align_bytes=64)
-                nc.scalar.activation(res[:], part[:], ACT.Relu, bias=qn_cols[:, h : h + 1])
+                qn_col = qn_cols[:, h : h + 1]
+                if (c, h) != (1, 1):
+                    part = sb.tile([P, HALF], F32, name="part%d%d" % (c, h), align_bytes=64)
+                    nc.vector.scalar_tensor_tensor(
+                        part[:], acc[:], -2.0, kn_rows[c][:], ALU.mult, ALU.add
+                    )
+                    nc.scalar.activation(res[:], part[:], ACT.Relu, bias=qn_col)
+                else:
+                    parts = []
+                    for j in range(2):
+                        cols = slice(P * j, P * (j + 1))
+                        part = sb.tile([P, P], F32, name="last%d" % j, align_bytes=64)
+                        nc.vector.scalar_tensor_tensor(
+                            part[:], acc[:, cols], -2.0, kn_rows[c][:, cols], ALU.mult, ALU.add
+                        )
+                        parts.append(part)
+                    for j in range(2):
+                        nc.vector.tensor_scalar(
+                            res[:, P * j : P * (j + 1)], parts[j][:], qn_col, 0.0, ALU.add, ALU.max
+                        )
                 nc.sync.dma_start(out[0, P * h : P * (h + 1), slots], res[:])

@@ -118,23 +118,20 @@ def tile_attend_infodist_topk_kernel(tc, qT, k_words, k_scales, kn, qn, offs, ou
                 )
                 res = sb.tile([P, HALF], F32, name="res%d%d" % (c, h), align_bytes=64)
                 qn_col = qn_cols[:, h : h + 1]
-                if (c, h) != (1, 1):
-                    part = sb.tile([P, HALF], F32, name="part%d%d" % (c, h), align_bytes=64)
+                parts = []
+                for j in range(2):
+                    cols = slice(P * j, P * (j + 1))
+                    part = sb.tile([P, P], F32, name="part%d%d%d" % (c, h, j), align_bytes=64)
                     nc.vector.scalar_tensor_tensor(
-                        part[:], acc[:], -2.0, kn_rows[c][:], ALU.mult, ALU.add
+                        part[:], acc[:, cols], -2.0, kn_rows[c][:, cols], ALU.mult, ALU.add
                     )
-                    nc.scalar.activation(res[:], part[:], ACT.Relu, bias=qn_col)
-                else:
-                    parts = []
-                    for j in range(2):
-                        cols = slice(P * j, P * (j + 1))
-                        part = sb.tile([P, P], F32, name="last%d" % j, align_bytes=64)
-                        nc.vector.scalar_tensor_tensor(
-                            part[:], acc[:, cols], -2.0, kn_rows[c][:, cols], ALU.mult, ALU.add
-                        )
-                        parts.append(part)
-                    for j in range(2):
+                    parts.append(part)
+                for j in range(2):
+                    cols = slice(P * j, P * (j + 1))
+                    if (c, h) != (1, 1):
+                        nc.scalar.activation(res[:, cols], parts[j][:], ACT.Relu, bias=qn_col)
+                    else:
                         nc.vector.tensor_scalar(
-                            res[:, P * j : P * (j + 1)], parts[j][:], qn_col, 0.0, ALU.add, ALU.max
+                            res[:, cols], parts[j][:], qn_col, 0.0, ALU.add, ALU.max
                         )
                 nc.sync.dma_start(out[0, P * h : P * (h + 1), slots], res[:])

@@ -106,16 +106,20 @@ def tile_attend_infodist_topk_kernel(tc, qT, k_words, k_scales, kn, qn, offs, ou
         for c in range(2):
             slots = slice(c * HALF, (c + 1) * HALF)
             for h in range(2):
-                acc = ps.tile([P, HALF], F32, name="acc%d%d" % (c, h))
-                nc.tensor.matmul_mx(
-                    out=acc[:],
-                    lhsT=q_codes[:, P * h : P * (h + 1)].bitcast(FP8X4),
-                    lhsT_scale=q_plane[:, P * h : P * (h + 1)],
-                    rhs=k_codes[c][:].bitcast(FP8X4),
-                    rhs_scale=k_planes[:, slots],
-                    start=True,
-                    stop=True,
-                )
+                width = P if (c, h) == (0, 0) else HALF
+                sums = []
+                for lo in range(0, HALF, width):
+                    acc = ps.tile([P, width], F32, name="acc%d%d%d" % (c, h, lo))
+                    nc.tensor.matmul_mx(
+                        out=acc[:],
+                        lhsT=q_codes[:, P * h : P * (h + 1)].bitcast(FP8X4),
+                        lhsT_scale=q_plane[:, P * h : P * (h + 1)],
+                        rhs=k_codes[c][:, lo : lo + width].bitcast(FP8X4),
+                        rhs_scale=k_planes[:, c * HALF + lo : c * HALF + lo + width],
+                        start=True,
+                        stop=True,
+                    )
+                    sums.extend(acc[:, j : j + P] for j in range(0, width, P))
                 res = sb.tile([P, HALF], F32, name="res%d%d" % (c, h), align_bytes=64)
                 qn_col = qn_cols[:, h : h + 1]
                 parts = []
@@ -123,7 +127,7 @@ def tile_attend_infodist_topk_kernel(tc, qT, k_words, k_scales, kn, qn, offs, ou
                     cols = slice(P * j, P * (j + 1))
                     part = sb.tile([P, P], F32, name="part%d%d%d" % (c, h, j), align_bytes=64)
                     nc.vector.scalar_tensor_tensor(
-                        part[:], acc[:, cols], -2.0, kn_rows[c][:, cols], ALU.mult, ALU.add
+                        part[:], sums[j], -2.0, kn_rows[c][:, cols], ALU.mult, ALU.add
                     )
                     parts.append(part)
                 for j in range(2):

@@ -78,14 +78,14 @@ def tile_attend_infodist_topk_kernel(tc, qT, k_words, k_scales, kn, qn, offs, ou
             in_=grouped[:].rearrange("p m j -> p (m j)"),
         )
 
-        turned = ps.tile([P, 4, P], F32, name="turned")
+        turned = ps.tile([P, 4, P], F32, name="turned", tag="bank5")
         for j in range(4):
             nc.tensor.transpose(turned[:, j, :], kn_listed[:, P * j : P * (j + 1)], ident[:])
         kn_cols = sb.tile([P, 4], F32, name="kn_cols", tag="q_raw", align_bytes=64)
         nc.scalar.copy(kn_cols[:], turned[:, :, KN_ROW])
         kn_rows = []
         for c in range(2):
-            spread = ps.tile([P, HALF], F32, name="spread%d" % c)
+            spread = ps.tile([P, HALF], F32, name="spread%d" % c, tag="bank%d" % (6 + c))
             for j in range(2):
                 nc.tensor.transpose(
                     spread[:, P * j : P * (j + 1)],
@@ -106,20 +106,20 @@ def tile_attend_infodist_topk_kernel(tc, qT, k_words, k_scales, kn, qn, offs, ou
         for c in range(2):
             slots = slice(c * HALF, (c + 1) * HALF)
             for h in range(2):
-                width = P if (c, h) == (0, 0) else HALF
                 sums = []
-                for lo in range(0, HALF, width):
-                    acc = ps.tile([P, width], F32, name="acc%d%d%d" % (c, h, lo))
+                for j in range(2):
+                    bank = 4 * c + 2 * h + j
+                    acc = ps.tile([P, P], F32, name="acc%d" % bank, tag="bank%d" % bank)
                     nc.tensor.matmul_mx(
                         out=acc[:],
                         lhsT=q_codes[:, P * h : P * (h + 1)].bitcast(FP8X4),
                         lhsT_scale=q_plane[:, P * h : P * (h + 1)],
-                        rhs=k_codes[c][:, lo : lo + width].bitcast(FP8X4),
-                        rhs_scale=k_planes[:, c * HALF + lo : c * HALF + lo + width],
+                        rhs=k_codes[c][:, P * j : P * (j + 1)].bitcast(FP8X4),
+                        rhs_scale=k_planes[:, c * HALF + P * j : c * HALF + P * (j + 1)],
                         start=True,
                         stop=True,
                     )
-                    sums.extend(acc[:, j : j + P] for j in range(0, width, P))
+                    sums.append(acc[:])
                 res = sb.tile([P, HALF], F32, name="res%d%d" % (c, h), align_bytes=64)
                 qn_col = qn_cols[:, h : h + 1]
                 parts = []

@@ -21,6 +21,7 @@ P = 128
 PACK = 4
 HALF = N // 2
 KN_ROW = P - 1
+SCALAR_ROWS = 32
 
 
 def tile_attend_infodist_topk_kernel(tc, qT, k_words, k_scales, kn, qn, offs, out):
@@ -33,7 +34,7 @@ def tile_attend_infodist_topk_kernel(tc, qT, k_words, k_scales, kn, qn, offs, ou
         scale_pool = sb.tile([P, T], U8, name="scale_pool", align_bytes=64)
         kn_pool = sb.tile([P, T], F32, name="kn_pool", align_bytes=64)
         word_pool = sb.tile([P, T], U32, name="word_pool", align_bytes=64)
-        q_raw = sb.tile([P, PACK, NQ], F32, name="q_raw", tag="q_raw", align_bytes=64)
+        q_raw = sb.tile([P, PACK, NQ], F32, name="q_raw", align_bytes=64)
         qn_cols = sb.tile([P, 2], F32, name="qn_cols")
         ident = sb.tile([P, P], F32, name="ident", align_bytes=64)
 
@@ -42,13 +43,13 @@ def tile_attend_infodist_topk_kernel(tc, qT, k_words, k_scales, kn, qn, offs, ou
         nc.vector.memset(ident[:], 0.0)
         make_identity(nc, ident[:], nomemset=True)
 
-        nc.sync.dma_start(kn_pool[KN_ROW:P, :], kn[0:1, :])
-        nc.sync.dma_start(offsets[:], offs)
         nc.sync.dma_start(q_raw[:], qT[0].rearrange("(p j) q -> p j q", j=PACK))
-        for quad in range(4):
+        nc.sync.dma_start(offsets[:], offs)
+        nc.sync.dma_start(kn_pool[KN_ROW:P, :], kn[0:1, :])
+        for r in range(4):
             nc.sync.dma_start(
-                scale_pool[32 * quad : 32 * quad + 4, :].bitcast(I32),
-                k_scales[0, 4 * quad : 4 * quad + 4, :].bitcast(I32),
+                scale_pool[r:P:32, :].bitcast(I32),
+                k_scales[0, r:16:4, :].bitcast(I32),
             )
         nc.sync.dma_start(
             word_pool[:].bitcast(I32),
@@ -57,19 +58,28 @@ def tile_attend_infodist_topk_kernel(tc, qT, k_words, k_scales, kn, qn, offs, ou
         with nc.allow_non_contiguous_dma(reason="one number a query row"):
             nc.sync.dma_start(qn_cols[:], qn[0].rearrange("(h m) o -> m (h o)", h=2))
 
-        kn_listed = sb.tile([P, N], F32, name="kn_listed", align_bytes=64)
-        nc.vector.tensor_copy(kn_listed[:], kn_pool[:].indirect(offsets[:]))
+        grouped = sb.tile([P, NQ, PACK], BF16, name="grouped", align_bytes=64)
+        rows = slice(0, SCALAR_ROWS)
+        nc.scalar.activation(
+            grouped[:, rows, :].rearrange("p (c i) j -> p c j i", i=4),
+            q_raw[:, :, rows].rearrange("p j (c i) -> p c j i", i=4),
+            ACT.Copy,
+        )
+        rows = slice(SCALAR_ROWS, NQ)
+        nc.vector.tensor_copy(
+            grouped[:, rows, :].rearrange("p (c i) j -> p c j i", i=4),
+            q_raw[:, :, rows].rearrange("p j (c i) -> p c j i", i=4),
+        )
+
+        kn_listed = []
+        for c in range(2):
+            listed = sb.tile([P, HALF], F32, name="kn_listed%d" % c, align_bytes=64)
+            cols = slice(c * (HALF // 16), (c + 1) * (HALF // 16))
+            nc.scalar.activation(listed[:], kn_pool[:].indirect(offsets[:, cols]), ACT.Copy)
+            kn_listed.append(listed)
         k_planes = sb.tile([P, N], U8, name="k_planes", align_bytes=64)
         nc.vector.tensor_copy(k_planes[:], scale_pool[:].indirect(offsets[:]))
 
-        grouped = sb.tile([P, NQ, PACK], BF16, name="grouped", align_bytes=64)
-        for h in range(2):
-            rows = slice(P * h, P * (h + 1))
-            nc.scalar.activation(
-                grouped[:, rows, :].rearrange("p (c i) j -> p c j i", i=4),
-                q_raw[:, :, rows].rearrange("p j (c i) -> p c j i", i=4),
-                ACT.Copy,
-            )
         q_codes = sb.tile([P, NQ], U32, name="q_codes", align_bytes=64)
         q_plane = sb.tile([P, NQ], U8, name="q_plane", align_bytes=64)
         nc.vector.quantize_mx(
@@ -78,18 +88,21 @@ def tile_attend_infodist_topk_kernel(tc, qT, k_words, k_scales, kn, qn, offs, ou
             in_=grouped[:].rearrange("p m j -> p (m j)"),
         )
 
-        turned = ps.tile([P, 4, P], F32, name="turned", tag="bank5")
-        for j in range(4):
-            nc.tensor.transpose(turned[:, j, :], kn_listed[:, P * j : P * (j + 1)], ident[:])
-        kn_cols = sb.tile([P, 4], F32, name="kn_cols", tag="q_raw", align_bytes=64)
-        nc.scalar.copy(kn_cols[:], turned[:, :, KN_ROW])
+        kn_cols = []
+        for c in range(2):
+            turned = ps.tile([P, 2, P], F32, name="turned%d" % c, tag="bank%d" % (4 + c))
+            for j in range(2):
+                nc.tensor.transpose(turned[:, j, :], kn_listed[c][:, P * j : P * (j + 1)], ident[:])
+            cols = sb.tile([P, 2], F32, name="kn_cols%d" % c)
+            nc.scalar.copy(cols[:], turned[:, :, KN_ROW])
+            kn_cols.append(cols)
         kn_rows = []
         for c in range(2):
             spread = ps.tile([P, HALF], F32, name="spread%d" % c, tag="bank%d" % (6 + c))
             for j in range(2):
                 nc.tensor.transpose(
                     spread[:, P * j : P * (j + 1)],
-                    kn_cols[:, 2 * c + j : 2 * c + j + 1].to_broadcast([P, P]),
+                    kn_cols[c][:, j : j + 1].to_broadcast([P, P]),
                     ident[:],
                 )
             rows = sb.tile([P, HALF], F32, name="kn_rows%d" % c, align_bytes=64)

@@ -22,6 +22,7 @@ PACK = 4
 HALF = N // 2
 KN_ROW = P - 1
 SCALAR_ROWS = 32
+LATE = 96
 
 
 def tile_attend_infodist_topk_kernel(tc, qT, k_words, k_scales, kn, qn, offs, out):
@@ -34,7 +35,13 @@ def tile_attend_infodist_topk_kernel(tc, qT, k_words, k_scales, kn, qn, offs, ou
         scale_pool = sb.tile([P, T], U8, name="scale_pool", align_bytes=64)
         kn_pool = sb.tile([P, T], F32, name="kn_pool", align_bytes=64)
         word_pool = sb.tile([P, T], U32, name="word_pool", align_bytes=64)
-        q_raw = sb.tile([P, PACK, NQ], F32, name="q_raw", align_bytes=64)
+        q_early = sb.tile([P, PACK, P], F32, name="q_early", align_bytes=64)
+        q_late = sb.tile([P, PACK * P], F32, name="q_late", tag="q_late", align_bytes=64)
+        cuts = [slice(0, LATE), slice(LATE, P)]
+        late = [
+            q_late[:, PACK * rows.start : PACK * rows.stop].rearrange("p (j q) -> p j q", j=PACK)
+            for rows in cuts
+        ]
         qn_cols = sb.tile([P, 2], F32, name="qn_cols")
         ident = sb.tile([P, P], F32, name="ident", align_bytes=64)
 
@@ -43,7 +50,8 @@ def tile_attend_infodist_topk_kernel(tc, qT, k_words, k_scales, kn, qn, offs, ou
         nc.vector.memset(ident[:], 0.0)
         make_identity(nc, ident[:], nomemset=True)
 
-        nc.sync.dma_start(q_raw[:], qT[0].rearrange("(p j) q -> p j q", j=PACK))
+        q_rows = qT[0].rearrange("(p j) q -> p j q", j=PACK)
+        nc.sync.dma_start(q_early[:], q_rows[:, :, 0:P])
         nc.sync.dma_start(offsets[:], offs)
         nc.sync.dma_start(kn_pool[KN_ROW:P, :], kn[0:1, :])
         for r in range(4):
@@ -55,42 +63,49 @@ def tile_attend_infodist_topk_kernel(tc, qT, k_words, k_scales, kn, qn, offs, ou
             word_pool[:].bitcast(I32),
             k_words[0].rearrange("p n t -> p (n t)").bitcast(I32),
         )
+        for u in range(2):
+            nc.sync.dma_start(late[u], q_rows[:, :, P + cuts[u].start : P + cuts[u].stop])
         with nc.allow_non_contiguous_dma(reason="one number a query row"):
             nc.sync.dma_start(qn_cols[:], qn[0].rearrange("(h m) o -> m (h o)", h=2))
 
-        grouped = sb.tile([P, NQ, PACK], BF16, name="grouped", align_bytes=64)
+        grouped = [sb.tile([P, P, PACK], BF16, name="grouped%d" % h, align_bytes=64) for h in range(2)]
+        q_codes = [sb.tile([P, P], U32, name="q_codes%d" % h, align_bytes=64) for h in range(2)]
+        q_plane = [sb.tile([P, P], U8, name="q_plane%d" % h, align_bytes=64) for h in range(2)]
+
+        def by_lines(h, rows, raw):
+            return (
+                grouped[h][:, rows, :].rearrange("p (c i) j -> p c j i", i=4),
+                raw.rearrange("p j (c i) -> p c j i", i=4),
+            )
+
+        def quantise(h):
+            nc.vector.quantize_mx(
+                out=q_codes[h][:].bitcast(FP8X4),
+                scales=q_plane[h][:],
+                in_=grouped[h][:].rearrange("p m j -> p (m j)"),
+            )
+
         rows = slice(0, SCALAR_ROWS)
-        nc.scalar.activation(
-            grouped[:, rows, :].rearrange("p (c i) j -> p c j i", i=4),
-            q_raw[:, :, rows].rearrange("p j (c i) -> p c j i", i=4),
-            ACT.Copy,
-        )
-        rows = slice(SCALAR_ROWS, NQ)
-        nc.vector.tensor_copy(
-            grouped[:, rows, :].rearrange("p (c i) j -> p c j i", i=4),
-            q_raw[:, :, rows].rearrange("p j (c i) -> p c j i", i=4),
-        )
+        nc.scalar.activation(*by_lines(0, rows, q_early[:, :, rows]), ACT.Copy)
+        rows = slice(SCALAR_ROWS, P)
+        nc.vector.tensor_copy(*by_lines(0, rows, q_early[:, :, rows]))
 
         kn_listed = []
         for c in range(2):
             listed = sb.tile([P, HALF], F32, name="kn_listed%d" % c, align_bytes=64)
             cols = slice(c * (HALF // 16), (c + 1) * (HALF // 16))
-            nc.scalar.activation(listed[:], kn_pool[:].indirect(offsets[:, cols]), ACT.Copy)
+            if c == 0:
+                nc.scalar.activation(listed[:], kn_pool[:].indirect(offsets[:, cols]), ACT.Copy)
+            else:
+                nc.vector.tensor_copy(listed[:], kn_pool[:].indirect(offsets[:, cols]))
             kn_listed.append(listed)
         k_planes = sb.tile([P, N], U8, name="k_planes", align_bytes=64)
         nc.vector.tensor_copy(k_planes[:], scale_pool[:].indirect(offsets[:]))
-
-        q_codes = sb.tile([P, NQ], U32, name="q_codes", align_bytes=64)
-        q_plane = sb.tile([P, NQ], U8, name="q_plane", align_bytes=64)
-        nc.vector.quantize_mx(
-            out=q_codes[:].bitcast(FP8X4),
-            scales=q_plane[:],
-            in_=grouped[:].rearrange("p m j -> p (m j)"),
-        )
+        quantise(0)
 
         kn_cols = []
         for c in range(2):
-            turned = ps.tile([P, 2, P], F32, name="turned%d" % c, tag="bank%d" % (4 + c))
+            turned = ps.tile([P, 2, P], F32, name="turned%d" % c, tag="bank%d" % (3 - 3 * c))
             for j in range(2):
                 nc.tensor.transpose(turned[:, j, :], kn_listed[c][:, P * j : P * (j + 1)], ident[:])
             cols = sb.tile([P, 2], F32, name="kn_cols%d" % c)
@@ -98,7 +113,7 @@ def tile_attend_infodist_topk_kernel(tc, qT, k_words, k_scales, kn, qn, offs, ou
             kn_cols.append(cols)
         kn_rows = []
         for c in range(2):
-            spread = ps.tile([P, HALF], F32, name="spread%d" % c, tag="bank%d" % (6 + c))
+            spread = ps.tile([P, HALF], F32, name="spread%d" % c, tag="bank%d" % (1 + c))
             for j in range(2):
                 nc.tensor.transpose(
                     spread[:, P * j : P * (j + 1)],
@@ -116,39 +131,48 @@ def tile_attend_infodist_topk_kernel(tc, qT, k_words, k_scales, kn, qn, offs, ou
             nc.vector.tensor_copy(listed[:], word_pool[:].indirect(offsets[:, cols]))
             k_codes.append(listed)
 
-        for c in range(2):
-            slots = slice(c * HALF, (c + 1) * HALF)
-            for h in range(2):
-                sums = []
+        for u in range(2):
+            nc.scalar.activation(*by_lines(1, cuts[u], late[u]), ACT.Copy)
+        quantise(1)
+
+        pair = ps.tile([P, 2, P], F32, name="acc2", tag="bank2")
+        banks = [ps.tile([P, P], F32, name="acc%d" % b, tag="bank%d" % b)[:] for b in range(2)]
+        banks = banks + [pair[:, 0, :], pair[:, 1, :]]
+        banks = banks + [ps.tile([P, P], F32, name="acc%d" % b, tag="bank%d" % b)[:] for b in range(3, 7)]
+        held = sb.tile([P, 3, P], F32, name="held", tag="q_late", align_bytes=64)
+        free = sb.tile([P, 5, P], F32, name="free", align_bytes=64)
+        parts = [free[:, 0, :]] + [held[:, b, :] for b in range(3)]
+        parts = parts + [free[:, b, :] for b in range(1, 5)]
+
+        for h in range(2):
+            for c in range(2):
+                slots = slice(c * HALF, (c + 1) * HALF)
                 for j in range(2):
-                    bank = 4 * c + 2 * h + j
-                    acc = ps.tile([P, P], F32, name="acc%d" % bank, tag="bank%d" % bank)
                     nc.tensor.matmul_mx(
-                        out=acc[:],
-                        lhsT=q_codes[:, P * h : P * (h + 1)].bitcast(FP8X4),
-                        lhsT_scale=q_plane[:, P * h : P * (h + 1)],
+                        out=banks[4 * h + 2 * c + j],
+                        lhsT=q_codes[h][:].bitcast(FP8X4),
+                        lhsT_scale=q_plane[h][:],
                         rhs=k_codes[c][:, P * j : P * (j + 1)].bitcast(FP8X4),
                         rhs_scale=k_planes[:, c * HALF + P * j : c * HALF + P * (j + 1)],
                         start=True,
                         stop=True,
                     )
-                    sums.append(acc[:])
                 res = sb.tile([P, HALF], F32, name="res%d%d" % (c, h), align_bytes=64)
                 qn_col = qn_cols[:, h : h + 1]
-                parts = []
                 for j in range(2):
-                    cols = slice(P * j, P * (j + 1))
-                    part = sb.tile([P, P], F32, name="part%d%d%d" % (c, h, j), align_bytes=64)
                     nc.vector.scalar_tensor_tensor(
-                        part[:], sums[j], -2.0, kn_rows[c][:, cols], ALU.mult, ALU.add
+                        parts[4 * h + 2 * c + j],
+                        banks[4 * h + 2 * c + j],
+                        -2.0,
+                        kn_rows[c][:, P * j : P * (j + 1)],
+                        ALU.mult,
+                        ALU.add,
                     )
-                    parts.append(part)
                 for j in range(2):
                     cols = slice(P * j, P * (j + 1))
+                    part = parts[4 * h + 2 * c + j]
                     if (c, h) != (1, 1):
-                        nc.scalar.activation(res[:, cols], parts[j][:], ACT.Relu, bias=qn_col)
+                        nc.scalar.activation(res[:, cols], part, ACT.Relu, bias=qn_col)
                     else:
-                        nc.vector.tensor_scalar(
-                            res[:, cols], parts[j][:], qn_col, 0.0, ALU.add, ALU.max
-                        )
+                        nc.vector.tensor_scalar(res[:, cols], part, qn_col, 0.0, ALU.add, ALU.max)
                 nc.sync.dma_start(out[0, P * h : P * (h + 1), slots], res[:])

@@ -21,37 +21,35 @@ P = 128
 PACK = 4
 HALF = N // 2
 KN_ROW = P - 1
-SCALAR_ROWS = 32
 LATE = 96
+EDGE = 48
 
 
 def tile_attend_infodist_topk_kernel(tc, qT, k_words, k_scales, kn, qn, offs, out):
     nc = tc.nc
     with ExitStack() as ctx:
         sb = ctx.enter_context(tc.tile_pool(name="sb", bufs=1))
+        reuse = ctx.enter_context(tc.tile_pool(name="reuse", bufs=1))
         ps = ctx.enter_context(tc.psum_pool(name="ps", bufs=1))
 
         offsets = sb.tile([P, N // 16], U16, name="offsets")
         scale_pool = sb.tile([P, T], U8, name="scale_pool", align_bytes=64)
-        kn_pool = sb.tile([P, T], F32, name="kn_pool", align_bytes=64)
-        word_pool = sb.tile([P, T], U32, name="word_pool", align_bytes=64)
+        kn_pool = sb.tile([P, T], F32, name="kn_pool", tag="window", align_bytes=64)
+        zeros = reuse.tile([P, EDGE], F32, name="zeros", offset=4 * T - 64, align_bytes=64)
         q_early = sb.tile([P, PACK, P], F32, name="q_early", align_bytes=64)
-        q_late = sb.tile([P, PACK * P], F32, name="q_late", tag="q_late", align_bytes=64)
-        cuts = [slice(0, LATE), slice(LATE, P)]
-        late = [
-            q_late[:, PACK * rows.start : PACK * rows.stop].rearrange("p (j q) -> p j q", j=PACK)
-            for rows in cuts
-        ]
-        qn_cols = sb.tile([P, 2], F32, name="qn_cols")
         ident = sb.tile([P, P], F32, name="ident", align_bytes=64)
 
+        nc.vector.memset(zeros[:], 0.0)
         nc.vector.memset(scale_pool[:].bitcast(I32), 0)
+        nc.vector.tensor_copy(ident[:, 0:EDGE], zeros[:])
+        zero_col = sb.tile([P, 1], F32, name="zero_col")
+        nc.vector.memset(zero_col[:], 0.0)
         nc.vector.memset(kn_pool[0:KN_ROW, :].bitcast(I32), 0)
-        nc.vector.memset(ident[:], 0.0)
+        nc.scalar.activation(ident[:, EDGE:P], zero_col[:].to_broadcast([P, P - EDGE]), ACT.Copy)
         make_identity(nc, ident[:], nomemset=True)
 
         q_rows = qT[0].rearrange("(p j) q -> p j q", j=PACK)
-        nc.sync.dma_start(q_early[:], q_rows[:, :, 0:P])
+        nc.scalar.dma_start(q_early[:], q_rows[:, :, 0:P])
         nc.sync.dma_start(offsets[:], offs)
         nc.sync.dma_start(kn_pool[KN_ROW:P, :], kn[0:1, :])
         for r in range(4):
@@ -59,6 +57,14 @@ def tile_attend_infodist_topk_kernel(tc, qT, k_words, k_scales, kn, qn, offs, ou
                 scale_pool[r:P:32, :].bitcast(I32),
                 k_scales[0, r:16:4, :].bitcast(I32),
             )
+        word_pool = reuse.tile([P, T], U32, name="word_pool", offset=0, align_bytes=64)
+        qn_cols = reuse.tile([P, 2], F32, name="qn_cols", offset=4 * T, align_bytes=64)
+        q_late = reuse.tile([P, PACK * P], F32, name="q_late", offset=4 * T + 64, align_bytes=64)
+        cuts = [slice(0, LATE), slice(LATE, P)]
+        late = [
+            q_late[:, PACK * rows.start : PACK * rows.stop].rearrange("p (j q) -> p j q", j=PACK)
+            for rows in cuts
+        ]
         nc.sync.dma_start(
             word_pool[:].bitcast(I32),
             k_words[0].rearrange("p n t -> p (n t)").bitcast(I32),
@@ -68,7 +74,7 @@ def tile_attend_infodist_topk_kernel(tc, qT, k_words, k_scales, kn, qn, offs, ou
         with nc.allow_non_contiguous_dma(reason="one number a query row"):
             nc.sync.dma_start(qn_cols[:], qn[0].rearrange("(h m) o -> m (h o)", h=2))
 
-        grouped = [sb.tile([P, P, PACK], BF16, name="grouped%d" % h, align_bytes=64) for h in range(2)]
+        grouped = [None, sb.tile([P, P, PACK], BF16, name="grouped1", align_bytes=64)]
         q_codes = [sb.tile([P, P], U32, name="q_codes%d" % h, align_bytes=64) for h in range(2)]
         q_plane = [sb.tile([P, P], U8, name="q_plane%d" % h, align_bytes=64) for h in range(2)]
 
@@ -85,11 +91,6 @@ def tile_attend_infodist_topk_kernel(tc, qT, k_words, k_scales, kn, qn, offs, ou
                 in_=grouped[h][:].rearrange("p m j -> p (m j)"),
             )
 
-        rows = slice(0, SCALAR_ROWS)
-        nc.scalar.activation(*by_lines(0, rows, q_early[:, :, rows]), ACT.Copy)
-        rows = slice(SCALAR_ROWS, P)
-        nc.vector.tensor_copy(*by_lines(0, rows, q_early[:, :, rows]))
-
         kn_listed = []
         for c in range(2):
             listed = sb.tile([P, HALF], F32, name="kn_listed%d" % c, align_bytes=64)
@@ -101,6 +102,8 @@ def tile_attend_infodist_topk_kernel(tc, qT, k_words, k_scales, kn, qn, offs, ou
             kn_listed.append(listed)
         k_planes = sb.tile([P, N], U8, name="k_planes", align_bytes=64)
         nc.vector.tensor_copy(k_planes[:], scale_pool[:].indirect(offsets[:]))
+        grouped[0] = sb.tile([P, P, PACK], BF16, name="grouped0", tag="window", align_bytes=64)
+        nc.vector.tensor_copy(*by_lines(0, slice(0, P), q_early[:]))
         quantise(0)
 
         kn_cols = []
@@ -139,7 +142,7 @@ def tile_attend_infodist_topk_kernel(tc, qT, k_words, k_scales, kn, qn, offs, ou
         banks = [ps.tile([P, P], F32, name="acc%d" % b, tag="bank%d" % b)[:] for b in range(2)]
         banks = banks + [pair[:, 0, :], pair[:, 1, :]]
         banks = banks + [ps.tile([P, P], F32, name="acc%d" % b, tag="bank%d" % b)[:] for b in range(3, 7)]
-        held = sb.tile([P, 3, P], F32, name="held", tag="q_late", align_bytes=64)
+        held = reuse.tile([P, 3, P], F32, name="held", offset=4 * T + 64, align_bytes=64)
         free = sb.tile([P, 5, P], F32, name="free", align_bytes=64)
         parts = [free[:, 0, :]] + [held[:, b, :] for b in range(3)]
         parts = parts + [free[:, b, :] for b in range(1, 5)]

@@ -33,7 +33,7 @@ def tile_attend_infodist_topk_kernel(tc, qT, k_words, k_scales, kn, qn, offs, ou
         ps = ctx.enter_context(tc.psum_pool(name="ps", bufs=1))
 
         offsets = sb.tile([P, N // 16], U16, name="offsets")
-        scale_pool = sb.tile([P, T], U8, name="scale_pool", align_bytes=64)
+        scale_pool = sb.tile([P, T], U8, name="scale_pool", tag="scales", align_bytes=64)
         kn_pool = sb.tile([P, T], F32, name="kn_pool", tag="window", align_bytes=64)
         zeros = reuse.tile([P, EDGE], F32, name="zeros", offset=4 * T - 64, align_bytes=64)
         q_early = sb.tile([P, PACK, P], F32, name="q_early", align_bytes=64)
@@ -75,7 +75,7 @@ def tile_attend_infodist_topk_kernel(tc, qT, k_words, k_scales, kn, qn, offs, ou
             nc.sync.dma_start(qn_cols[:], qn[0].rearrange("(h m) o -> m (h o)", h=2))
 
         grouped = [None, sb.tile([P, P, PACK], BF16, name="grouped1", align_bytes=64)]
-        q_codes = [sb.tile([P, P], U32, name="q_codes%d" % h, align_bytes=64) for h in range(2)]
+        q_codes = [None, sb.tile([P, P], U32, name="q_codes1", align_bytes=64)]
         q_plane = [sb.tile([P, P], U8, name="q_plane%d" % h, align_bytes=64) for h in range(2)]
 
         def by_lines(h, rows, raw):
@@ -103,7 +103,8 @@ def tile_attend_infodist_topk_kernel(tc, qT, k_words, k_scales, kn, qn, offs, ou
         k_planes = sb.tile([P, N], U8, name="k_planes", align_bytes=64)
         nc.vector.tensor_copy(k_planes[:], scale_pool[:].indirect(offsets[:]))
         grouped[0] = sb.tile([P, P, PACK], BF16, name="grouped0", tag="window", align_bytes=64)
-        nc.vector.tensor_copy(*by_lines(0, slice(0, P), q_early[:]))
+        nc.scalar.activation(*by_lines(0, slice(0, P), q_early[:]), ACT.Copy)
+        q_codes[0] = sb.tile([P, P], U32, name="q_codes0", tag="scales", align_bytes=64)
         quantise(0)
 
         kn_cols = []

@@ -43,17 +43,18 @@ def tile_attend_infodist_topk_kernel(tc, qT, k_words, k_scales, kn, qn, offs, ou
         nc.vector.memset(scale_pool[:].bitcast(I32), 0)
         nc.vector.tensor_copy(ident[:, 0:EDGE], zeros[:])
         zero_col = sb.tile([P, 1], F32, name="zero_col")
-        nc.vector.memset(zero_col[:], 0.0)
         nc.vector.memset(kn_pool[0:KN_ROW, :].bitcast(I32), 0)
+        nc.vector.memset(zero_col[:], 0.0)
         nc.scalar.activation(ident[:, EDGE:P], zero_col[:].to_broadcast([P, P - EDGE]), ACT.Copy)
         make_identity(nc, ident[:], nomemset=True)
 
         q_rows = qT[0].rearrange("(p j) q -> p j q", j=PACK)
-        nc.scalar.dma_start(q_early[:], q_rows[:, :, 0:P])
+        nc.sync.dma_start(q_early[:], q_rows[:, :, 0:P])
         nc.sync.dma_start(offsets[:], offs)
-        nc.sync.dma_start(kn_pool[KN_ROW:P, :], kn[0:1, :])
+        nc.scalar.dma_start(kn_pool[KN_ROW:P, :], kn[0:1, :])
         for r in range(4):
-            nc.sync.dma_start(
+            queue = nc.scalar if r == 3 else nc.sync
+            queue.dma_start(
                 scale_pool[r:P:32, :].bitcast(I32),
                 k_scales[0, r:16:4, :].bitcast(I32),
             )
@@ -74,7 +75,7 @@ def tile_attend_infodist_topk_kernel(tc, qT, k_words, k_scales, kn, qn, offs, ou
         with nc.allow_non_contiguous_dma(reason="one number a query row"):
             nc.sync.dma_start(qn_cols[:], qn[0].rearrange("(h m) o -> m (h o)", h=2))
 
-        grouped = [None, sb.tile([P, P, PACK], BF16, name="grouped1", align_bytes=64)]
+        grouped = [None, None]
         q_codes = [None, sb.tile([P, P], U32, name="q_codes1", align_bytes=64)]
         q_plane = [sb.tile([P, P], U8, name="q_plane%d" % h, align_bytes=64) for h in range(2)]
 
@@ -112,7 +113,7 @@ def tile_attend_infodist_topk_kernel(tc, qT, k_words, k_scales, kn, qn, offs, ou
             turned = ps.tile([P, 2, P], F32, name="turned%d" % c, tag="bank%d" % (3 - 3 * c))
             for j in range(2):
                 nc.tensor.transpose(turned[:, j, :], kn_listed[c][:, P * j : P * (j + 1)], ident[:])
-            cols = sb.tile([P, 2], F32, name="kn_cols%d" % c)
+            cols = sb.tile([P, 2], F32, name="kn_cols%d" % c, tag="cols%d" % c, align_bytes=64)
             nc.scalar.copy(cols[:], turned[:, :, KN_ROW])
             kn_cols.append(cols)
         kn_rows = []
@@ -135,6 +136,7 @@ def tile_attend_infodist_topk_kernel(tc, qT, k_words, k_scales, kn, qn, offs, ou
             nc.vector.tensor_copy(listed[:], word_pool[:].indirect(offsets[:, cols]))
             k_codes.append(listed)
 
+        grouped[1] = sb.tile([P, P, PACK], BF16, name="grouped1", tag="cols1", align_bytes=64)
         for u in range(2):
             nc.scalar.activation(*by_lines(1, cuts[u], late[u]), ACT.Copy)
         quantise(1)

@@ -23,6 +23,7 @@ HALF = N // 2
 KN_ROW = P - 1
 LATE = 96
 EDGE = 48
+SCALES_AT = 6 * T
 
 
 def tile_attend_infodist_topk_kernel(tc, qT, k_words, k_scales, kn, qn, offs, out):
@@ -33,7 +34,7 @@ def tile_attend_infodist_topk_kernel(tc, qT, k_words, k_scales, kn, qn, offs, ou
         ps = ctx.enter_context(tc.psum_pool(name="ps", bufs=1))
 
         offsets = sb.tile([P, N // 16], U16, name="offsets")
-        scale_pool = sb.tile([P, T], U8, name="scale_pool", tag="scales", align_bytes=64)
+        scale_pool = reuse.tile([P, T], U8, name="scale_pool", offset=SCALES_AT, align_bytes=64)
         kn_pool = sb.tile([P, T], F32, name="kn_pool", tag="window", align_bytes=64)
         zeros = reuse.tile([P, EDGE], F32, name="zeros", offset=4 * T - 64, align_bytes=64)
         q_early = sb.tile([P, PACK, P], F32, name="q_early", align_bytes=64)
@@ -45,15 +46,13 @@ def tile_attend_infodist_topk_kernel(tc, qT, k_words, k_scales, kn, qn, offs, ou
         zero_col = sb.tile([P, 1], F32, name="zero_col")
         nc.vector.memset(kn_pool[0:KN_ROW, :].bitcast(I32), 0)
         nc.vector.memset(zero_col[:], 0.0)
-        nc.scalar.activation(ident[:, EDGE:P], zero_col[:].to_broadcast([P, P - EDGE]), ACT.Copy)
-        make_identity(nc, ident[:], nomemset=True)
 
         q_rows = qT[0].rearrange("(p j) q -> p j q", j=PACK)
         nc.sync.dma_start(q_early[:], q_rows[:, :, 0:P])
         nc.sync.dma_start(offsets[:], offs)
         nc.scalar.dma_start(kn_pool[KN_ROW:P, :], kn[0:1, :])
         for r in range(4):
-            queue = nc.scalar if r == 3 else nc.sync
+            queue = nc.scalar if r >= 2 else nc.sync
             queue.dma_start(
                 scale_pool[r:P:32, :].bitcast(I32),
                 k_scales[0, r:16:4, :].bitcast(I32),
@@ -74,6 +73,9 @@ def tile_attend_infodist_topk_kernel(tc, qT, k_words, k_scales, kn, qn, offs, ou
             nc.sync.dma_start(late[u], q_rows[:, :, P + cuts[u].start : P + cuts[u].stop])
         with nc.allow_non_contiguous_dma(reason="one number a query row"):
             nc.sync.dma_start(qn_cols[:], qn[0].rearrange("(h m) o -> m (h o)", h=2))
+
+        nc.scalar.activation(ident[:, EDGE:P], zero_col[:].to_broadcast([P, P - EDGE]), ACT.Copy)
+        make_identity(nc, ident[:], nomemset=True)
 
         grouped = [None, None]
         q_codes = [None, sb.tile([P, P], U32, name="q_codes1", align_bytes=64)]
@@ -105,7 +107,7 @@ def tile_attend_infodist_topk_kernel(tc, qT, k_words, k_scales, kn, qn, offs, ou
         nc.vector.tensor_copy(k_planes[:], scale_pool[:].indirect(offsets[:]))
         grouped[0] = sb.tile([P, P, PACK], BF16, name="grouped0", tag="window", align_bytes=64)
         nc.scalar.activation(*by_lines(0, slice(0, P), q_early[:]), ACT.Copy)
-        q_codes[0] = sb.tile([P, P], U32, name="q_codes0", tag="scales", align_bytes=64)
+        q_codes[0] = reuse.tile([P, P], U32, name="q_codes0", offset=SCALES_AT, align_bytes=64)
         quantise(0)
 
         kn_cols = []
@@ -131,7 +133,8 @@ def tile_attend_infodist_topk_kernel(tc, qT, k_words, k_scales, kn, qn, offs, ou
 
         k_codes = []
         for c in range(2):
-            listed = sb.tile([P, HALF], U32, name="k_codes%d" % c, align_bytes=64)
+            at = SCALES_AT + 4 * (P + c * HALF)
+            listed = reuse.tile([P, HALF], U32, name="k_codes%d" % c, offset=at, align_bytes=64)
             cols = slice(c * (HALF // 16), (c + 1) * (HALF // 16))
             nc.vector.tensor_copy(listed[:], word_pool[:].indirect(offsets[:, cols]))
             k_codes.append(listed)
@@ -145,10 +148,9 @@ def tile_attend_infodist_topk_kernel(tc, qT, k_words, k_scales, kn, qn, offs, ou
         banks = [ps.tile([P, P], F32, name="acc%d" % b, tag="bank%d" % b)[:] for b in range(2)]
         banks = banks + [pair[:, 0, :], pair[:, 1, :]]
         banks = banks + [ps.tile([P, P], F32, name="acc%d" % b, tag="bank%d" % b)[:] for b in range(3, 7)]
-        held = reuse.tile([P, 3, P], F32, name="held", offset=4 * T + 64, align_bytes=64)
-        free = sb.tile([P, 5, P], F32, name="free", align_bytes=64)
-        parts = [free[:, 0, :]] + [held[:, b, :] for b in range(3)]
-        parts = parts + [free[:, b, :] for b in range(1, 5)]
+        held = reuse.tile([P, 4, P], F32, name="held", offset=4 * T + 64, align_bytes=64)
+        free = sb.tile([P, 4, P], F32, name="free", align_bytes=64)
+        parts = [held[:, b, :] for b in range(4)] + [free[:, b, :] for b in range(4)]
 
         for h in range(2):
             for c in range(2):

@@ -48,11 +48,11 @@ def tile_attend_infodist_topk_kernel(tc, qT, k_words, k_scales, kn, qn, offs, ou
         nc.vector.memset(zero_col[:], 0.0)
 
         q_rows = qT[0].rearrange("(p j) q -> p j q", j=PACK)
-        nc.sync.dma_start(q_early[:], q_rows[:, :, 0:P])
         nc.sync.dma_start(offsets[:], offs)
+        nc.sync.dma_start(q_early[:], q_rows[:, :, 0:P])
         nc.scalar.dma_start(kn_pool[KN_ROW:P, :], kn[0:1, :])
         for r in range(4):
-            queue = nc.scalar if r >= 2 else nc.sync
+            queue = nc.scalar if r == 3 else nc.sync
             queue.dma_start(
                 scale_pool[r:P:32, :].bitcast(I32),
                 k_scales[0, r:16:4, :].bitcast(I32),

@@ -22,7 +22,6 @@ PACK = 4
 HALF = N // 2
 KN_ROW = P - 1
 LATE = 96
-EDGE = 48
 SCALES_AT = 6 * T
 
 
@@ -36,21 +35,21 @@ def tile_attend_infodist_topk_kernel(tc, qT, k_words, k_scales, kn, qn, offs, ou
         offsets = sb.tile([P, N // 16], U16, name="offsets")
         scale_pool = reuse.tile([P, T], U8, name="scale_pool", offset=SCALES_AT, align_bytes=64)
         kn_pool = sb.tile([P, T], F32, name="kn_pool", tag="window", align_bytes=64)
-        zeros = reuse.tile([P, EDGE], F32, name="zeros", offset=4 * T - 64, align_bytes=64)
         q_early = sb.tile([P, PACK, P], F32, name="q_early", align_bytes=64)
         ident = sb.tile([P, P], F32, name="ident", align_bytes=64)
 
-        nc.vector.memset(zeros[:], 0.0)
-        nc.vector.memset(scale_pool[:].bitcast(I32), 0)
-        nc.vector.tensor_copy(ident[:, 0:EDGE], zeros[:])
         zero_col = sb.tile([P, 1], F32, name="zero_col")
-        nc.vector.memset(kn_pool[0:KN_ROW, :].bitcast(I32), 0)
+        for words in (scale_pool[:].bitcast(I32), kn_pool[0:KN_ROW, :].bitcast(I32)):
+            mid = words.shape[1] // 2
+            nc.vector.memset(words[:, 0 : mid - 1], 0)
+            nc.vector.memset(words[:, mid - 1 : mid], 0)
+            nc.gpsimd.memset(words[:, mid:], 0)
         nc.vector.memset(zero_col[:], 0.0)
 
         q_rows = qT[0].rearrange("(p j) q -> p j q", j=PACK)
         nc.sync.dma_start(offsets[:], offs)
+        nc.sync.dma_start(kn_pool[KN_ROW:P, :], kn[0:1, :])
         nc.sync.dma_start(q_early[:], q_rows[:, :, 0:P])
-        nc.scalar.dma_start(kn_pool[KN_ROW:P, :], kn[0:1, :])
         for r in range(4):
             queue = nc.scalar if r == 3 else nc.sync
             queue.dma_start(
@@ -74,7 +73,7 @@ def tile_attend_infodist_topk_kernel(tc, qT, k_words, k_scales, kn, qn, offs, ou
         with nc.allow_non_contiguous_dma(reason="one number a query row"):
             nc.sync.dma_start(qn_cols[:], qn[0].rearrange("(h m) o -> m (h o)", h=2))
 
-        nc.scalar.activation(ident[:, EDGE:P], zero_col[:].to_broadcast([P, P - EDGE]), ACT.Copy)
+        nc.scalar.activation(ident[:], zero_col[:].to_broadcast([P, P]), ACT.Copy)
         make_identity(nc, ident[:], nomemset=True)
 
         grouped = [None, None]

@@ -34,21 +34,20 @@ def tile_attend_infodist_topk_kernel(tc, qT, k_words, k_scales, kn, qn, offs, ou
 
         offsets = sb.tile([P, N // 16], U16, name="offsets")
         scale_pool = reuse.tile([P, T], U8, name="scale_pool", offset=SCALES_AT, align_bytes=64)
-        kn_pool = sb.tile([P, T], F32, name="kn_pool", tag="window", align_bytes=64)
+        kn_pool = sb.tile([P, T], F32, name="kn_pool", align_bytes=64)
         q_early = sb.tile([P, PACK, P], F32, name="q_early", align_bytes=64)
         ident = sb.tile([P, P], F32, name="ident", align_bytes=64)
 
-        zero_col = sb.tile([P, 1], F32, name="zero_col")
         for words in (scale_pool[:].bitcast(I32), kn_pool[0:KN_ROW, :].bitcast(I32)):
             mid = words.shape[1] // 2
             nc.vector.memset(words[:, 0 : mid - 1], 0)
             nc.vector.memset(words[:, mid - 1 : mid], 0)
             nc.gpsimd.memset(words[:, mid:], 0)
-        nc.vector.memset(zero_col[:], 0.0)
+        nc.vector.memset(ident[:], 0.0)
 
         q_rows = qT[0].rearrange("(p j) q -> p j q", j=PACK)
         nc.sync.dma_start(offsets[:], offs)
-        nc.sync.dma_start(kn_pool[KN_ROW:P, :], kn[0:1, :])
+        nc.scalar.dma_start(kn_pool[KN_ROW:P, :], kn[0:1, :])
         nc.sync.dma_start(q_early[:], q_rows[:, :, 0:P])
         for r in range(4):
             queue = nc.scalar if r == 3 else nc.sync
@@ -73,7 +72,6 @@ def tile_attend_infodist_topk_kernel(tc, qT, k_words, k_scales, kn, qn, offs, ou
         with nc.allow_non_contiguous_dma(reason="one number a query row"):
             nc.sync.dma_start(qn_cols[:], qn[0].rearrange("(h m) o -> m (h o)", h=2))
 
-        nc.scalar.activation(ident[:], zero_col[:].to_broadcast([P, P]), ACT.Copy)
         make_identity(nc, ident[:], nomemset=True)
 
         grouped = [None, None]
@@ -97,14 +95,11 @@ def tile_attend_infodist_topk_kernel(tc, qT, k_words, k_scales, kn, qn, offs, ou
         for c in range(2):
             listed = sb.tile([P, HALF], F32, name="kn_listed%d" % c, align_bytes=64)
             cols = slice(c * (HALF // 16), (c + 1) * (HALF // 16))
-            if c == 0:
-                nc.scalar.activation(listed[:], kn_pool[:].indirect(offsets[:, cols]), ACT.Copy)
-            else:
-                nc.vector.tensor_copy(listed[:], kn_pool[:].indirect(offsets[:, cols]))
+            nc.vector.tensor_copy(listed[:], kn_pool[:].indirect(offsets[:, cols]))
             kn_listed.append(listed)
         k_planes = sb.tile([P, N], U8, name="k_planes", align_bytes=64)
         nc.vector.tensor_copy(k_planes[:], scale_pool[:].indirect(offsets[:]))
-        grouped[0] = sb.tile([P, P, PACK], BF16, name="grouped0", tag="window", align_bytes=64)
+        grouped[0] = sb.tile([P, P, PACK], BF16, name="grouped0", align_bytes=64)
         nc.scalar.activation(*by_lines(0, slice(0, P), q_early[:]), ACT.Copy)
         q_codes[0] = reuse.tile([P, P], U32, name="q_codes0", offset=SCALES_AT, align_bytes=64)
         quantise(0)

@@ -21,8 +21,11 @@ P = 128
 PACK = 4
 HALF = N // 2
 KN_ROW = P - 1
+SCALE_ROW = 48
+KN_CUT = 1024
 LATE = 96
-SCALES_AT = 6 * T
+CODES_AT = 4 * T
+COLS_AT = (CODES_AT + 4 * HALF, CODES_AT - 64)
 
 
 def tile_attend_infodist_topk_kernel(tc, qT, k_words, k_scales, kn, qn, offs, out):
@@ -33,88 +36,95 @@ def tile_attend_infodist_topk_kernel(tc, qT, k_words, k_scales, kn, qn, offs, ou
         ps = ctx.enter_context(tc.psum_pool(name="ps", bufs=1))
 
         offsets = sb.tile([P, N // 16], U16, name="offsets")
-        scale_pool = reuse.tile([P, T], U8, name="scale_pool", offset=SCALES_AT, align_bytes=64)
+        scale_pool = reuse.tile([P, T], U8, name="scale_pool", offset=0, align_bytes=64)
         kn_pool = sb.tile([P, T], F32, name="kn_pool", align_bytes=64)
         q_early = sb.tile([P, PACK, P], F32, name="q_early", align_bytes=64)
+        q_late = reuse.tile([P, PACK * P], F32, name="q_late", offset=2 * T, align_bytes=64)
+        word_pool = sb.tile([P, T], U32, name="word_pool", align_bytes=64)
         ident = sb.tile([P, P], F32, name="ident", align_bytes=64)
+        k_planes = sb.tile([P, N], U8, name="k_planes", align_bytes=64)
 
-        for words in (scale_pool[:].bitcast(I32), kn_pool[0:KN_ROW, :].bitcast(I32)):
-            mid = words.shape[1] // 2
-            nc.vector.memset(words[:, 0 : mid - 1], 0)
-            nc.vector.memset(words[:, mid - 1 : mid], 0)
-            nc.gpsimd.memset(words[:, mid:], 0)
-        nc.vector.memset(ident[:], 0.0)
-
-        q_rows = qT[0].rearrange("(p j) q -> p j q", j=PACK)
         nc.sync.dma_start(offsets[:], offs)
         nc.scalar.dma_start(kn_pool[KN_ROW:P, :], kn[0:1, :])
+        nc.sync.dma_start(
+            scale_pool[SCALE_ROW : SCALE_ROW + 16, :].bitcast(I32), k_scales[0].bitcast(I32)
+        )
+        q_rows = qT[0].rearrange("(p j) q -> p j q", j=PACK)
         nc.sync.dma_start(q_early[:], q_rows[:, :, 0:P])
-        for r in range(4):
-            queue = nc.scalar if r == 3 else nc.sync
-            queue.dma_start(
-                scale_pool[r:P:32, :].bitcast(I32),
-                k_scales[0, r:16:4, :].bitcast(I32),
-            )
-        word_pool = reuse.tile([P, T], U32, name="word_pool", offset=0, align_bytes=64)
-        qn_cols = reuse.tile([P, 2], F32, name="qn_cols", offset=4 * T, align_bytes=64)
-        q_late = reuse.tile([P, PACK * P], F32, name="q_late", offset=4 * T + 64, align_bytes=64)
+        nc.sync.dma_start(
+            word_pool[:].bitcast(I32),
+            k_words[0].rearrange("p n t -> p (n t)").bitcast(I32),
+        )
         cuts = [slice(0, LATE), slice(LATE, P)]
         late = [
             q_late[:, PACK * rows.start : PACK * rows.stop].rearrange("p (j q) -> p j q", j=PACK)
             for rows in cuts
         ]
-        nc.sync.dma_start(
-            word_pool[:].bitcast(I32),
-            k_words[0].rearrange("p n t -> p (n t)").bitcast(I32),
-        )
         for u in range(2):
             nc.sync.dma_start(late[u], q_rows[:, :, P + cuts[u].start : P + cuts[u].stop])
+
+        zero = sb.tile([P, 1], F32, name="zero")
+        nc.gpsimd.memset(zero[:], 0.0)
+        nc.scalar.activation(ident[:], zero[:].to_broadcast([P, P]), ACT.Copy)
+        nc.gpsimd.memset(scale_pool[SCALE_ROW + 16 : P, :].bitcast(I32), 0)
+        kn_words = kn_pool[0:KN_ROW, :].bitcast(I32)
+        for words in (scale_pool[0:SCALE_ROW, :].bitcast(I32), kn_words[:, 0:KN_CUT]):
+            last = words.shape[1] - 1
+            nc.vector.memset(words[:, 0:last], 0)
+            nc.vector.memset(words[:, last:], 0)
+        nc.gpsimd.memset(kn_words[:, KN_CUT:], 0)
+        make_identity(nc, ident[:], nomemset=True)
+        nc.gpsimd.memset(k_planes[:].bitcast(I32), 0)
+
+        scales_listed = sb.tile([P, N], U8, name="scales_listed", align_bytes=64)
+        nc.vector.tensor_copy(scales_listed[:], scale_pool[:].indirect(offsets[:]))
+        for r in range(4):
+            nc.sync.dma_start(
+                k_planes[r:P:32, :].bitcast(I32),
+                scales_listed[SCALE_ROW + r : SCALE_ROW + 16 : 4, :].bitcast(I32),
+            )
+        qn_cols = reuse.tile([P, 2], F32, name="qn_cols", offset=0, align_bytes=64)
         with nc.allow_non_contiguous_dma(reason="one number a query row"):
             nc.sync.dma_start(qn_cols[:], qn[0].rearrange("(h m) o -> m (h o)", h=2))
-
-        make_identity(nc, ident[:], nomemset=True)
-
-        grouped = [None, None]
-        q_codes = [None, sb.tile([P, P], U32, name="q_codes1", align_bytes=64)]
-        q_plane = [sb.tile([P, P], U8, name="q_plane%d" % h, align_bytes=64) for h in range(2)]
-
-        def by_lines(h, rows, raw):
-            return (
-                grouped[h][:, rows, :].rearrange("p (c i) j -> p c j i", i=4),
-                raw.rearrange("p j (c i) -> p c j i", i=4),
-            )
-
-        def quantise(h):
-            nc.vector.quantize_mx(
-                out=q_codes[h][:].bitcast(FP8X4),
-                scales=q_plane[h][:],
-                in_=grouped[h][:].rearrange("p m j -> p (m j)"),
-            )
 
         kn_listed = []
         for c in range(2):
             listed = sb.tile([P, HALF], F32, name="kn_listed%d" % c, align_bytes=64)
             cols = slice(c * (HALF // 16), (c + 1) * (HALF // 16))
-            nc.vector.tensor_copy(listed[:], kn_pool[:].indirect(offsets[:, cols]))
+            nc.scalar.activation(listed[:], kn_pool[:].indirect(offsets[:, cols]), ACT.Copy)
             kn_listed.append(listed)
-        k_planes = sb.tile([P, N], U8, name="k_planes", align_bytes=64)
-        nc.vector.tensor_copy(k_planes[:], scale_pool[:].indirect(offsets[:]))
-        grouped[0] = sb.tile([P, P, PACK], BF16, name="grouped0", align_bytes=64)
-        nc.scalar.activation(*by_lines(0, slice(0, P), q_early[:]), ACT.Copy)
-        q_codes[0] = reuse.tile([P, P], U32, name="q_codes0", offset=SCALES_AT, align_bytes=64)
-        quantise(0)
+
+        q_codes = [sb.tile([P, P], U32, name="q_codes%d" % h, align_bytes=64) for h in range(2)]
+        q_plane = [sb.tile([P, P], U8, name="q_plane%d" % h, align_bytes=64) for h in range(2)]
+
+        def by_lines(grouped, raw):
+            return (
+                grouped.rearrange("p (c i) j -> p c j i", i=4),
+                raw.rearrange("p j (c i) -> p c j i", i=4),
+            )
+
+        def quantise(h, grouped):
+            nc.vector.quantize_mx(
+                out=q_codes[h][:].bitcast(FP8X4),
+                scales=q_plane[h][:],
+                in_=grouped[:].rearrange("p m j -> p (m j)"),
+            )
+
+        grouped_early = sb.tile([P, P, PACK], BF16, name="grouped_early", align_bytes=64)
+        nc.vector.tensor_copy(*by_lines(grouped_early[:], q_early[:]))
+        quantise(0, grouped_early)
 
         kn_cols = []
         for c in range(2):
             turned = ps.tile([P, 2, P], F32, name="turned%d" % c, tag="bank%d" % (3 - 3 * c))
             for j in range(2):
                 nc.tensor.transpose(turned[:, j, :], kn_listed[c][:, P * j : P * (j + 1)], ident[:])
-            cols = sb.tile([P, 2], F32, name="kn_cols%d" % c, tag="cols%d" % c, align_bytes=64)
-            nc.scalar.copy(cols[:], turned[:, :, KN_ROW])
+            cols = reuse.tile([P, 32], F32, name="kn_cols%d" % c, offset=COLS_AT[c], align_bytes=64)
+            nc.scalar.copy(cols[:, 0:2], turned[:, :, KN_ROW])
             kn_cols.append(cols)
         kn_rows = []
         for c in range(2):
-            spread = ps.tile([P, HALF], F32, name="spread%d" % c, tag="bank%d" % (1 + c))
+            spread = ps.tile([P, HALF], F32, name="spread%d" % c, tag="bank%d" % (1 - c))
             for j in range(2):
                 nc.tensor.transpose(
                     spread[:, P * j : P * (j + 1)],
@@ -127,31 +137,26 @@ def tile_attend_infodist_topk_kernel(tc, qT, k_words, k_scales, kn, qn, offs, ou
 
         k_codes = []
         for c in range(2):
-            at = SCALES_AT + 4 * (P + c * HALF)
-            listed = reuse.tile([P, HALF], U32, name="k_codes%d" % c, offset=at, align_bytes=64)
+            listed = reuse.tile([P, HALF], U32, name="k_codes%d" % c, offset=CODES_AT + 4 * HALF * c, align_bytes=64)
             cols = slice(c * (HALF // 16), (c + 1) * (HALF // 16))
             nc.vector.tensor_copy(listed[:], word_pool[:].indirect(offsets[:, cols]))
             k_codes.append(listed)
 
-        grouped[1] = sb.tile([P, P, PACK], BF16, name="grouped1", tag="cols1", align_bytes=64)
+        grouped_late = reuse.tile([P, P, PACK], BF16, name="grouped_late", offset=CODES_AT - 1024, align_bytes=64)
         for u in range(2):
-            nc.scalar.activation(*by_lines(1, cuts[u], late[u]), ACT.Copy)
-        quantise(1)
-
-        pair = ps.tile([P, 2, P], F32, name="acc2", tag="bank2")
-        banks = [ps.tile([P, P], F32, name="acc%d" % b, tag="bank%d" % b)[:] for b in range(2)]
-        banks = banks + [pair[:, 0, :], pair[:, 1, :]]
-        banks = banks + [ps.tile([P, P], F32, name="acc%d" % b, tag="bank%d" % b)[:] for b in range(3, 7)]
-        held = reuse.tile([P, 4, P], F32, name="held", offset=4 * T + 64, align_bytes=64)
-        free = sb.tile([P, 4, P], F32, name="free", align_bytes=64)
-        parts = [held[:, b, :] for b in range(4)] + [free[:, b, :] for b in range(4)]
+            nc.scalar.activation(*by_lines(grouped_late[:, cuts[u], :], late[u]), ACT.Copy)
+        quantise(1, grouped_late)
+        held = reuse.tile([P, 2, HALF], F32, name="held", offset=2 * T, align_bytes=64)
+        free = sb.tile([P, 2, HALF], F32, name="free", align_bytes=64)
 
         for h in range(2):
             for c in range(2):
                 slots = slice(c * HALF, (c + 1) * HALF)
+                b = 2 * c + 4 * h
+                banks = [ps.tile([P, P], F32, name="acc%d" % (b + j), tag="bank%d" % (b + j)) for j in range(2)]
                 for j in range(2):
                     nc.tensor.matmul_mx(
-                        out=banks[4 * h + 2 * c + j],
+                        out=banks[j][:],
                         lhsT=q_codes[h][:].bitcast(FP8X4),
                         lhsT_scale=q_plane[h][:],
                         rhs=k_codes[c][:, P * j : P * (j + 1)].bitcast(FP8X4),
@@ -159,22 +164,18 @@ def tile_attend_infodist_topk_kernel(tc, qT, k_words, k_scales, kn, qn, offs, ou
                         start=True,
                         stop=True,
                     )
+                part = (held, free)[h][:, c, :]
                 res = sb.tile([P, HALF], F32, name="res%d%d" % (c, h), align_bytes=64)
                 qn_col = qn_cols[:, h : h + 1]
                 for j in range(2):
+                    cols = slice(P * j, P * (j + 1))
                     nc.vector.scalar_tensor_tensor(
-                        parts[4 * h + 2 * c + j],
-                        banks[4 * h + 2 * c + j],
-                        -2.0,
-                        kn_rows[c][:, P * j : P * (j + 1)],
-                        ALU.mult,
-                        ALU.add,
+                        part[:, cols], banks[j][:], -2.0, kn_rows[c][:, cols], ALU.mult, ALU.add
                     )
                 for j in range(2):
                     cols = slice(P * j, P * (j + 1))
-                    part = parts[4 * h + 2 * c + j]
                     if (c, h) != (1, 1):
-                        nc.scalar.activation(res[:, cols], part, ACT.Relu, bias=qn_col)
+                        nc.scalar.activation(res[:, cols], part[:, cols], ACT.Relu, bias=qn_col)
                     else:
-                        nc.vector.tensor_scalar(res[:, cols], part, qn_col, 0.0, ALU.add, ALU.max)
+                        nc.vector.tensor_scalar(res[:, cols], part[:, cols], qn_col, 0.0, ALU.add, ALU.max)
                 nc.sync.dma_start(out[0, P * h : P * (h + 1), slots], res[:])

@@ -22,10 +22,10 @@ PACK = 4
 HALF = N // 2
 KN_ROW = P - 1
 SCALE_ROW = 48
-KN_CUT = 1024
+KN_CUT = 1280
 LATE = 96
 CODES_AT = 4 * T
-COLS_AT = (CODES_AT + 4 * HALF, CODES_AT - 64)
+COLS_AT = (CODES_AT + 8 * HALF, CODES_AT - 64)
 
 
 def tile_attend_infodist_topk_kernel(tc, qT, k_words, k_scales, kn, qn, offs, out):
@@ -64,17 +64,24 @@ def tile_attend_infodist_topk_kernel(tc, qT, k_words, k_scales, kn, qn, offs, ou
             nc.sync.dma_start(late[u], q_rows[:, :, P + cuts[u].start : P + cuts[u].stop])
 
         zero = sb.tile([P, 1], F32, name="zero")
+        warm = sb.tile([P, 1], F32, name="warm")
         nc.gpsimd.memset(zero[:], 0.0)
-        nc.scalar.activation(ident[:], zero[:].to_broadcast([P, P]), ACT.Copy)
-        nc.gpsimd.memset(scale_pool[SCALE_ROW + 16 : P, :].bitcast(I32), 0)
+        nc.scalar.activation(warm[:], zero[:], ACT.Copy)
+        nc.gpsimd.memset(ident[:], 0.0)
+        nc.gpsimd.memset(k_planes[:].bitcast(I32), 0)
+        make_identity(nc, ident[:], nomemset=True)
         kn_words = kn_pool[0:KN_ROW, :].bitcast(I32)
-        for words in (scale_pool[0:SCALE_ROW, :].bitcast(I32), kn_words[:, 0:KN_CUT]):
+        nc.gpsimd.memset(kn_words[:, KN_CUT:], 0)
+        for words in (kn_words[:, 0:KN_CUT], scale_pool[0:SCALE_ROW, :].bitcast(I32)):
             last = words.shape[1] - 1
             nc.vector.memset(words[:, 0:last], 0)
             nc.vector.memset(words[:, last:], 0)
-        nc.gpsimd.memset(kn_words[:, KN_CUT:], 0)
-        make_identity(nc, ident[:], nomemset=True)
-        nc.gpsimd.memset(k_planes[:].bitcast(I32), 0)
+        nc.gpsimd.memset(scale_pool[SCALE_ROW + 16 : P, :].bitcast(I32), 0)
+
+        kn_listed = [sb.tile([P, HALF], F32, name="kn_listed%d" % c, align_bytes=64) for c in range(2)]
+        halves = [offsets[:, c * (HALF // 16) : (c + 1) * (HALF // 16)] for c in range(2)]
+        nc.scalar.activation(kn_listed[0][:], kn_pool[:].indirect(halves[0]), ACT.Copy)
+        nc.vector.tensor_copy(kn_listed[1][:], kn_pool[:].indirect(halves[1]))
 
         scales_listed = sb.tile([P, N], U8, name="scales_listed", align_bytes=64)
         nc.vector.tensor_copy(scales_listed[:], scale_pool[:].indirect(offsets[:]))
@@ -86,13 +93,6 @@ def tile_attend_infodist_topk_kernel(tc, qT, k_words, k_scales, kn, qn, offs, ou
         qn_cols = reuse.tile([P, 2], F32, name="qn_cols", offset=0, align_bytes=64)
         with nc.allow_non_contiguous_dma(reason="one number a query row"):
             nc.sync.dma_start(qn_cols[:], qn[0].rearrange("(h m) o -> m (h o)", h=2))
-
-        kn_listed = []
-        for c in range(2):
-            listed = sb.tile([P, HALF], F32, name="kn_listed%d" % c, align_bytes=64)
-            cols = slice(c * (HALF // 16), (c + 1) * (HALF // 16))
-            nc.scalar.activation(listed[:], kn_pool[:].indirect(offsets[:, cols]), ACT.Copy)
-            kn_listed.append(listed)
 
         q_codes = [sb.tile([P, P], U32, name="q_codes%d" % h, align_bytes=64) for h in range(2)]
         q_plane = [sb.tile([P, P], U8, name="q_plane%d" % h, align_bytes=64) for h in range(2)]
@@ -110,7 +110,7 @@ def tile_attend_infodist_topk_kernel(tc, qT, k_words, k_scales, kn, qn, offs, ou
                 in_=grouped[:].rearrange("p m j -> p (m j)"),
             )
 
-        grouped_early = sb.tile([P, P, PACK], BF16, name="grouped_early", align_bytes=64)
+        grouped_early = reuse.tile([P, P, PACK], BF16, name="grouped_early", offset=1024, align_bytes=64)
         nc.vector.tensor_copy(*by_lines(grouped_early[:], q_early[:]))
         quantise(0, grouped_early)
 
@@ -137,7 +137,7 @@ def tile_attend_infodist_topk_kernel(tc, qT, k_words, k_scales, kn, qn, offs, ou
 
         k_codes = []
         for c in range(2):
-            listed = reuse.tile([P, HALF], U32, name="k_codes%d" % c, offset=CODES_AT + 4 * HALF * c, align_bytes=64)
+            listed = reuse.tile([P, HALF], U32, name="k_codes%d" % c, offset=(1024, CODES_AT)[c], align_bytes=64)
             cols = slice(c * (HALF // 16), (c + 1) * (HALF // 16))
             nc.vector.tensor_copy(listed[:], word_pool[:].indirect(offsets[:, cols]))
             k_codes.append(listed)

@@ -1,7 +1,6 @@
 from contextlib import ExitStack
 
 import concourse.mybir as mybir
-from concourse.masks import make_identity
 
 N, T, D, NQ = 512, 2048, 512, 256
 FLOPS = 2 * NQ * N * D
@@ -22,7 +21,7 @@ PACK = 4
 HALF = N // 2
 KN_ROW = P - 1
 SCALE_ROW = 48
-KN_CUT = 1280
+KN_CUT = 1024
 LATE = 96
 CODES_AT = 4 * T
 COLS_AT = (CODES_AT + 8 * HALF, CODES_AT - 64)
@@ -63,13 +62,11 @@ def tile_attend_infodist_topk_kernel(tc, qT, k_words, k_scales, kn, qn, offs, ou
         for u in range(2):
             nc.sync.dma_start(late[u], q_rows[:, :, P + cuts[u].start : P + cuts[u].stop])
 
-        zero = sb.tile([P, 1], F32, name="zero")
-        warm = sb.tile([P, 1], F32, name="warm")
-        nc.gpsimd.memset(zero[:], 0.0)
-        nc.scalar.activation(warm[:], zero[:], ACT.Copy)
-        nc.gpsimd.memset(ident[:], 0.0)
-        nc.gpsimd.memset(k_planes[:].bitcast(I32), 0)
-        make_identity(nc, ident[:], nomemset=True)
+        apart = sb.tile([P, P], F32, name="apart", align_bytes=64)
+        distance = sb.tile([P, P], F32, name="distance", align_bytes=64)
+        nc.gpsimd.iota(apart[:], [[1, P]], base=0, channel_multiplier=-1, allow_small_or_imprecise_dtypes=True)
+        nc.scalar.activation(distance[:], apart[:], ACT.Abs)
+        nc.scalar.activation(ident[:], distance[:], ACT.Relu, bias=1.0, scale=-1.0)
         kn_words = kn_pool[0:KN_ROW, :].bitcast(I32)
         nc.gpsimd.memset(kn_words[:, KN_CUT:], 0)
         for words in (kn_words[:, 0:KN_CUT], scale_pool[0:SCALE_ROW, :].bitcast(I32)):
@@ -77,6 +74,7 @@ def tile_attend_infodist_topk_kernel(tc, qT, k_words, k_scales, kn, qn, offs, ou
             nc.vector.memset(words[:, 0:last], 0)
             nc.vector.memset(words[:, last:], 0)
         nc.gpsimd.memset(scale_pool[SCALE_ROW + 16 : P, :].bitcast(I32), 0)
+        nc.gpsimd.memset(k_planes[:].bitcast(I32), 0)
 
         kn_listed = [sb.tile([P, HALF], F32, name="kn_listed%d" % c, align_bytes=64) for c in range(2)]
         halves = [offsets[:, c * (HALF // 16) : (c + 1) * (HALF // 16)] for c in range(2)]

from contextlib import ExitStack

import concourse.mybir as mybir

N, T, D, NQ = 512, 2048, 512, 256
FLOPS = 2 * NQ * N * D
BYTES = 4 * D * NQ + D * T + 16 * T + 4 * T + 4 * NQ + 2 * 128 * (N // 16) + 4 * NQ * N

F32 = mybir.dt.float32
BF16 = mybir.dt.bfloat16
I32 = mybir.dt.int32
U32 = mybir.dt.uint32
U16 = mybir.dt.uint16
U8 = mybir.dt.uint8
FP8X4 = mybir.dt.float8_e4m3fn_x4
ALU = mybir.AluOpType
ACT = mybir.ActivationFunctionType

P = 128
PACK = 4
HALF = N // 2
KN_ROW = P - 1
SCALE_ROW = 48
KN_CUT = 1024
LATE = 96
CODES_AT = 4 * T
COLS_AT = (CODES_AT + 8 * HALF, CODES_AT - 64)


def tile_attend_infodist_topk_kernel(tc, qT, k_words, k_scales, kn, qn, offs, out):
    nc = tc.nc
    with ExitStack() as ctx:
        sb = ctx.enter_context(tc.tile_pool(name="sb", bufs=1))
        reuse = ctx.enter_context(tc.tile_pool(name="reuse", bufs=1))
        ps = ctx.enter_context(tc.psum_pool(name="ps", bufs=1))

        offsets = sb.tile([P, N // 16], U16, name="offsets")
        scale_pool = reuse.tile([P, T], U8, name="scale_pool", offset=0, align_bytes=64)
        kn_pool = sb.tile([P, T], F32, name="kn_pool", align_bytes=64)
        q_early = sb.tile([P, PACK, P], F32, name="q_early", align_bytes=64)
        q_late = reuse.tile([P, PACK * P], F32, name="q_late", offset=2 * T, align_bytes=64)
        word_pool = sb.tile([P, T], U32, name="word_pool", align_bytes=64)
        ident = sb.tile([P, P], F32, name="ident", align_bytes=64)
        k_planes = sb.tile([P, N], U8, name="k_planes", align_bytes=64)

        nc.sync.dma_start(offsets[:], offs)
        nc.scalar.dma_start(kn_pool[KN_ROW:P, :], kn[0:1, :])
        nc.sync.dma_start(
            scale_pool[SCALE_ROW : SCALE_ROW + 16, :].bitcast(I32), k_scales[0].bitcast(I32)
        )
        q_rows = qT[0].rearrange("(p j) q -> p j q", j=PACK)
        nc.sync.dma_start(q_early[:], q_rows[:, :, 0:P])
        nc.sync.dma_start(
            word_pool[:].bitcast(I32),
            k_words[0].rearrange("p n t -> p (n t)").bitcast(I32),
        )
        cuts = [slice(0, LATE), slice(LATE, P)]
        late = [
            q_late[:, PACK * rows.start : PACK * rows.stop].rearrange("p (j q) -> p j q", j=PACK)
            for rows in cuts
        ]
        for u in range(2):
            nc.sync.dma_start(late[u], q_rows[:, :, P + cuts[u].start : P + cuts[u].stop])

        apart = sb.tile([P, P], F32, name="apart", align_bytes=64)
        distance = sb.tile([P, P], F32, name="distance", align_bytes=64)
        nc.gpsimd.iota(apart[:], [[1, P]], base=0, channel_multiplier=-1, allow_small_or_imprecise_dtypes=True)
        nc.scalar.activation(distance[:], apart[:], ACT.Abs)
        nc.scalar.activation(ident[:], distance[:], ACT.Relu, bias=1.0, scale=-1.0)
        kn_words = kn_pool[0:KN_ROW, :].bitcast(I32)
        nc.gpsimd.memset(kn_words[:, KN_CUT:], 0)
        for words in (kn_words[:, 0:KN_CUT], scale_pool[0:SCALE_ROW, :].bitcast(I32)):
            last = words.shape[1] - 1
            nc.vector.memset(words[:, 0:last], 0)
            nc.vector.memset(words[:, last:], 0)
        nc.gpsimd.memset(scale_pool[SCALE_ROW + 16 : P, :].bitcast(I32), 0)
        nc.gpsimd.memset(k_planes[:].bitcast(I32), 0)

        kn_listed = [sb.tile([P, HALF], F32, name="kn_listed%d" % c, align_bytes=64) for c in range(2)]
        halves = [offsets[:, c * (HALF // 16) : (c + 1) * (HALF // 16)] for c in range(2)]
        nc.scalar.activation(kn_listed[0][:], kn_pool[:].indirect(halves[0]), ACT.Copy)
        nc.vector.tensor_copy(kn_listed[1][:], kn_pool[:].indirect(halves[1]))

        scales_listed = sb.tile([P, N], U8, name="scales_listed", align_bytes=64)
        nc.vector.tensor_copy(scales_listed[:], scale_pool[:].indirect(offsets[:]))
        for r in range(4):
            nc.sync.dma_start(
                k_planes[r:P:32, :].bitcast(I32),
                scales_listed[SCALE_ROW + r : SCALE_ROW + 16 : 4, :].bitcast(I32),
            )
        qn_cols = reuse.tile([P, 2], F32, name="qn_cols", offset=0, align_bytes=64)
        with nc.allow_non_contiguous_dma(reason="one number a query row"):
            nc.sync.dma_start(qn_cols[:], qn[0].rearrange("(h m) o -> m (h o)", h=2))

        q_codes = [sb.tile([P, P], U32, name="q_codes%d" % h, align_bytes=64) for h in range(2)]
        q_plane = [sb.tile([P, P], U8, name="q_plane%d" % h, align_bytes=64) for h in range(2)]

        def by_lines(grouped, raw):
            return (
                grouped.rearrange("p (c i) j -> p c j i", i=4),
                raw.rearrange("p j (c i) -> p c j i", i=4),
            )

        def quantise(h, grouped):
            nc.vector.quantize_mx(
                out=q_codes[h][:].bitcast(FP8X4),
                scales=q_plane[h][:],
                in_=grouped[:].rearrange("p m j -> p (m j)"),
            )

        grouped_early = reuse.tile([P, P, PACK], BF16, name="grouped_early", offset=1024, align_bytes=64)
        nc.vector.tensor_copy(*by_lines(grouped_early[:], q_early[:]))
        quantise(0, grouped_early)

        kn_cols = []
        for c in range(2):
            turned = ps.tile([P, 2, P], F32, name="turned%d" % c, tag="bank%d" % (3 - 3 * c))
            for j in range(2):
                nc.tensor.transpose(turned[:, j, :], kn_listed[c][:, P * j : P * (j + 1)], ident[:])
            cols = reuse.tile([P, 32], F32, name="kn_cols%d" % c, offset=COLS_AT[c], align_bytes=64)
            nc.scalar.copy(cols[:, 0:2], turned[:, :, KN_ROW])
            kn_cols.append(cols)
        kn_rows = []
        for c in range(2):
            spread = ps.tile([P, HALF], F32, name="spread%d" % c, tag="bank%d" % (1 - c))
            for j in range(2):
                nc.tensor.transpose(
                    spread[:, P * j : P * (j + 1)],
                    kn_cols[c][:, j : j + 1].to_broadcast([P, P]),
                    ident[:],
                )
            rows = sb.tile([P, HALF], F32, name="kn_rows%d" % c, align_bytes=64)
            nc.scalar.copy(rows[:], spread[:])
            kn_rows.append(rows)

        k_codes = []
        for c in range(2):
            listed = reuse.tile([P, HALF], U32, name="k_codes%d" % c, offset=(1024, CODES_AT)[c], align_bytes=64)
            cols = slice(c * (HALF // 16), (c + 1) * (HALF // 16))
            nc.vector.tensor_copy(listed[:], word_pool[:].indirect(offsets[:, cols]))
            k_codes.append(listed)

        grouped_late = reuse.tile([P, P, PACK], BF16, name="grouped_late", offset=CODES_AT - 1024, align_bytes=64)
        for u in range(2):
            nc.scalar.activation(*by_lines(grouped_late[:, cuts[u], :], late[u]), ACT.Copy)
        quantise(1, grouped_late)
        held = reuse.tile([P, 2, HALF], F32, name="held", offset=2 * T, align_bytes=64)
        free = sb.tile([P, 2, HALF], F32, name="free", align_bytes=64)

        for h in range(2):
            for c in range(2):
                slots = slice(c * HALF, (c + 1) * HALF)
                b = 2 * c + 4 * h
                banks = [ps.tile([P, P], F32, name="acc%d" % (b + j), tag="bank%d" % (b + j)) for j in range(2)]
                for j in range(2):
                    nc.tensor.matmul_mx(
                        out=banks[j][:],
                        lhsT=q_codes[h][:].bitcast(FP8X4),
                        lhsT_scale=q_plane[h][:],
                        rhs=k_codes[c][:, P * j : P * (j + 1)].bitcast(FP8X4),
                        rhs_scale=k_planes[:, c * HALF + P * j : c * HALF + P * (j + 1)],
                        start=True,
                        stop=True,
                    )
                part = (held, free)[h][:, c, :]
                res = sb.tile([P, HALF], F32, name="res%d%d" % (c, h), align_bytes=64)
                qn_col = qn_cols[:, h : h + 1]
                for j in range(2):
                    cols = slice(P * j, P * (j + 1))
                    nc.vector.scalar_tensor_tensor(
                        part[:, cols], banks[j][:], -2.0, kn_rows[c][:, cols], ALU.mult, ALU.add
                    )
                for j in range(2):
                    cols = slice(P * j, P * (j + 1))
                    if (c, h) != (1, 1):
                        nc.scalar.activation(res[:, cols], part[:, cols], ACT.Relu, bias=qn_col)
                    else:
                        nc.vector.tensor_scalar(res[:, cols], part[:, cols], qn_col, 0.0, ALU.add, ALU.max)
                nc.sync.dma_start(out[0, P * h : P * (h + 1), slots], res[:])
